import numpy as np
import ml_dtypes


def mxq(x, axis, fmt="e4m3"):
    dtype, down = {"e4m3": (ml_dtypes.float8_e4m3fn, 7), "e5m2": (ml_dtypes.float8_e5m2, 14)}[fmt]
    v = np.moveaxis(np.asarray(x, np.float32).astype(ml_dtypes.bfloat16).astype(np.float64), axis, -1)
    blocks = v.reshape(v.shape[:-1] + (-1, 32))
    amax = np.abs(blocks).max(-1, keepdims=True)
    byte = np.maximum(np.where(amax > 0, np.frexp(amax)[1] - 1 + 127, 0) - down, 1)
    scale = np.exp2(byte - 127.0)
    codes = (blocks / scale).astype(np.float32).astype(dtype).astype(np.float64)
    return np.moveaxis((codes * scale).reshape(v.shape), -1, axis)


WIDE = False


def mx_kscale(k):
    if not WIDE:
        return np.ones(k)
    levels = np.array([10, -10, 5, -5, 0])
    if k % 512:
        return np.exp2(np.random.permutation(np.resize(levels, k // 32))).repeat(32)
    a = np.empty((k // 512, 16))
    for p in range(k // 512):
        a[p, :8] = np.random.permutation(np.resize(levels, 8))
        for g in range(8):
            far = levels[np.abs(levels - a[p, g]) >= 10]
            a[p, g + 8] = far[np.random.randint(len(far))]
    return np.exp2(a.ravel()).repeat(32)


def f64(x):
    return np.asarray(x).astype(np.float64)


def striped(idx):
    return np.tile(idx.reshape(-1, 16).T, (8, 1)).astype(np.uint16)


def unstriped(offs):
    return offs[:16].T.reshape(-1).astype(np.int64)


E2M1 = np.array([0.0, 0.5, 1.0, 1.5, 2.0, 3.0, 4.0, 6.0, -0.0, -0.5, -1.0, -1.5, -2.0, -3.0, -4.0, -6.0])


def pack_weight(w, fmt):
    k, n = w.shape
    w = f64(np.asarray(w, np.float32).astype(ml_dtypes.bfloat16)).reshape(k // 32, 32, n)
    amax = np.abs(w).max(1)
    if fmt == "e4m3":
        byte = np.frexp(amax)[1] - 1 + 127 - 7
    else:
        mant, ex = np.frexp(amax / 6.0)
        byte = np.where(mant > 0.5, ex, ex - 1) + 127
    byte = np.clip(np.where(amax > 0, byte, 1), 1, 254)
    scaled = (w * np.exp2(127.0 - byte)[:, None, :]).reshape(k, n).astype(np.float32)
    by_word = np.ascontiguousarray(scaled.reshape(k // 512, 128, 4, n).transpose(0, 1, 3, 2))
    if fmt == "e4m3":
        words = by_word.astype(ml_dtypes.float8_e4m3fn).view(np.uint8)
    else:
        c = by_word.astype(ml_dtypes.float4_e2m1fn).view(np.uint8) & 0xF
        words = (c[..., 0::2] | (c[..., 1::2] << 4)).reshape(k // 512, 128, 2 * n)
    return np.ascontiguousarray(words), np.ascontiguousarray(byte.astype(np.uint8).reshape(k // 512, 16, n))


def unpack_weight(words, scales, fmt):
    g, _, n = scales.shape
    words = np.ascontiguousarray(words).reshape(g, 128, n, -1)
    if fmt == "e4m3":
        vals = words.view(ml_dtypes.float8_e4m3fn).astype(np.float64)
    else:
        nib = np.empty((g, 128, n, 4), np.uint8)
        nib[..., 0::2] = words & 0xF
        nib[..., 1::2] = words >> 4
        vals = E2M1[nib]
    vals = vals * np.repeat(np.exp2(scales.astype(np.float64) - 127.0), 8, axis=1)[..., None]
    return vals.transpose(0, 1, 3, 2).reshape(g * 512, n)


def gelu(v):
    return 0.5 * v * (1.0 + np.tanh(np.sqrt(2.0 / np.pi) * (v + 0.044715 * v**3)))


def striped8(idx):
    return np.concatenate([v.reshape(-1, 16).T for v in idx]).astype(np.uint16)


def unstriped8(offs):
    return np.stack([offs[16 * g:16 * g + 16].T.reshape(-1) for g in range(8)]).astype(np.int64)


def heads(xT, wgt, idx8):
    k = np.arange(xT.shape[0])
    return wgt[k // 4 % 128] * xT[k[:, None], idx8[k % 512 // 64]]


K, D, H, N, T, V, S, R, P = 1024, 512, 1024, 512, 2048, 2048, 1024, 8, 16

def setup_inputs():
    n = np.random.standard_normal
    s = mx_kscale(K)[:, None]
    q = mx_kscale(D)[:, None]
    u = mx_kscale(H)[:, None]
    tab_words, tab_scales = pack_weight(n((D, V)) * q, "e4m3")
    wt_words, wt_scales = pack_weight(n((D, H)) / np.sqrt(D) / q * u.T, "e2m1")
    wo_words, wo_scales = pack_weight(n((H, N)) / np.sqrt(H) / u, "e4m3")
    return {
        "xT": (n((K, T)) * s).astype(np.float32),
        "wgt": np.repeat(np.random.uniform(0.5, 2.0, (R, S)), P, axis=0).astype(np.float32),
        "offs2": striped8(np.stack([np.random.permutation(T)[:S] for _ in range(R)])),
        "tab_words": tab_words, "tab_scales": tab_scales,
        "offs": striped(np.random.permutation(V)[:S]),
        "wx": (n((K, H)) / np.sqrt(K) / s * u.T).astype(np.float32),
        "bx": (0.5 * n(H) * u[:, 0]).astype(np.float32),
        "wt_words": wt_words, "wt_scales": wt_scales,
        "wo_words": wo_words, "wo_scales": wo_scales,
        "bo": (0.5 * n(N)).astype(np.float32),
        "old": n((N, S)).astype(np.float32),
    }

def reference(xT, wgt, offs2, tab_words, tab_scales, offs, wx, bx, wt_words, wt_scales, wo_words, wo_scales, bo, old):
    xg = heads(f64(xT), f64(wgt), unstriped8(offs2))
    v = unpack_weight(tab_words, tab_scales, "e4m3")[:, unstriped(offs)]
    wt = unpack_weight(wt_words, wt_scales, "e2m1")
    wo = unpack_weight(wo_words, wo_scales, "e4m3")
    a = mxq(f64(wx), 0, "e4m3").T @ mxq(xg, 0, "e4m3")
    p = wt.T @ v
    h = np.maximum(a + f64(bx)[:, None], p)
    y = wo.T @ mxq(h, 0, "e4m3")
    return f64(old) + np.tanh(y + f64(bo)[:, None])

@@ -1,0 +1,335 @@
+from contextlib import ExitStack
+
+import concourse.mybir as mybir
+
+K, D, H, N, T, V, S = 1024, 512, 1024, 512, 2048, 2048, 1024
+FLOPS = 2 * S * (K * H + D * H + H * N)
+
+F32 = mybir.dt.float32
+BF16 = mybir.dt.bfloat16
+I32 = mybir.dt.int32
+U32 = mybir.dt.uint32
+U16 = mybir.dt.uint16
+U8 = mybir.dt.uint8
+FP8X4 = mybir.dt.float8_e4m3fn_x4
+FP4X4 = mybir.dt.float4_e2m1fn_x4
+ALU = mybir.AluOpType
+ACT = mybir.ActivationFunctionType
+
+P = 128
+PACK = 4
+KP = P * PACK
+CH = 512
+NCH = S // CH
+LCOL = CH // 16
+
+
+def tile_list_relation_type_max_kernel(
+    tc, xT, wgt, offs2, tab_words, tab_scales, offs, wx, bx, wt_words, wt_scales, wo_words, wo_scales, bo, old, out
+):
+    nc = tc.nc
+    with ExitStack() as ctx:
+        lists = ctx.enter_context(tc.tile_pool(name="lists", bufs=1))
+        keep = ctx.enter_context(tc.tile_pool(name="keep", bufs=1))
+        ring = ctx.enter_context(tc.tile_pool(name="ring", bufs=2))
+        psum = ctx.enter_context(tc.psum_pool(name="psum", bufs=1))
+
+        def kept(name, shape, dtype):
+            return keep.tile(shape, dtype, name=name, align_bytes=64)
+
+        offs2_sb = lists.tile([P, S // 16], U16, name="offs2_sb")
+        offs_sb = lists.tile([P, S // 16], U16, name="offs_sb")
+
+        wt_sc_raw = kept("wt_sc_raw", [P, H // 4], I32)
+        tab_sc = kept("tab_sc", [P, V // 4], I32)
+        wo_sc = kept("wo_sc", [P, 2, N // 4], I32)
+        nc.vector.memset(tab_sc[:], 0)
+        nc.vector.memset(wt_sc_raw[:], 0)
+        nc.vector.memset(wo_sc[:], 0)
+        warm = kept("warm", [P, 1], F32)
+        nc.vector.memset(warm[:], 0.0)
+        warm_out = kept("warm_out", [P, 1], F32)
+        nc.scalar.activation(warm_out[:], warm[:], ACT.Tanh)
+        bx_sb = kept("bx_sb", [P, 2, PACK], F32)
+        bo_sb = kept("bo_sb", [P, N // P], F32)
+
+        def load_scale_rows(queue, tile, rows):
+            for q in range(4):
+                queue.dma_start(tile[32 * q : 32 * q + 4], rows[4 * q : 4 * q + 4].bitcast(I32))
+
+        wt_raw = kept("wt_raw", [P, H // 2], I32)
+        wgt_sb = kept("wgt_sb", [P, S], F32)
+        tab_w = kept("tab_w", [P, V], I32)
+        wo_w = kept("wo_w", [P, 2, N], I32)
+        old_sb = {}
+        planes = {}
+        wx_raw = {}
+
+        def load_plane(a, i):
+            planes[a, i] = ring.tile([P, T], F32, name="plane", bufs=8)
+            rows = xT[KP * a : KP * (a + 1), :].rearrange("(p i) t -> p i t", i=PACK)
+            nc.sync.dma_start(planes[a, i][:], rows[:, i, :])
+
+        def load_wx(a, b):
+            wx_raw[a, b] = ring.tile([P, PACK, KP], F32, name="wx_raw", bufs=4)
+            rows = wx[KP * a : KP * (a + 1), KP * b : KP * (b + 1)].rearrange("(p j) c -> p j c", j=PACK)
+            nc.sync.dma_start(wx_raw[a, b][:], rows)
+
+        wq = {}
+
+        def cast_wx(a, b, engine):
+            wb = ring.tile([P, KP * PACK], BF16, name="b16", bufs=7, align_bytes=64)
+            dst = wb[:].rearrange("p (t m j) -> p m j t", t=PACK, j=PACK)
+            src = wx_raw[a, b][:].rearrange("p j (m t) -> p m j t", t=PACK)
+            if engine == "scalar":
+                nc.scalar.copy(dst, src)
+            else:
+                nc.vector.tensor_copy(dst, src)
+            return wb
+
+        def quantize(name, src):
+            codes = kept(name + "_c", [P, src.shape[1] // PACK], U32)
+            scales = kept(name + "_s", [P, src.shape[1] // PACK], U8)
+            nc.vector.quantize_mx(out=codes[:].bitcast(FP8X4), scales=scales[:], in_=src)
+            return codes, scales
+
+        g = {}
+
+        def gather(a, i, c, lo=0, hi=CH):
+            if (a, c) not in g:
+                g[a, c] = ring.tile([P, PACK, CH], F32, name="f32x4", bufs=5)
+            nc.vector.tensor_tensor(
+                g[a, c][:, i, lo:hi],
+                planes[a, i][:].indirect(offs2_sb[:, (CH * c + lo) // 16 : (CH * c + hi) // 16]),
+                wgt_sb[:, CH * c + lo : CH * c + hi],
+                ALU.mult,
+            )
+
+        xb = {}
+
+        def interleave(a, c, lo, hi, engine):
+            if (a, c) not in xb:
+                xb[a, c] = ring.tile([P, CH * PACK], BF16, name="b16", bufs=7, align_bytes=64)
+            dst = xb[a, c][:, PACK * lo : PACK * hi].rearrange("p (c i t) -> p c t i", i=4, t=PACK)
+            src = g[a, c][:, :, lo:hi].rearrange("p t (c i) -> p c t i", i=4)
+            if engine == "scalar":
+                nc.scalar.copy(dst, src)
+            else:
+                nc.vector.tensor_copy(dst, src)
+
+        def interleave_pair(a, c, u, lo, hi):
+            if (a, c) not in xb:
+                xb[a, c] = ring.tile([P, CH * PACK], BF16, name="b16", bufs=7, align_bytes=64)
+            dst = xb[a, c][:, PACK * lo : PACK * hi].rearrange("p (n t) -> p n t", t=PACK)[:, :, 2 * u : 2 * u + 2]
+            src = g[a, c][:, 2 * u : 2 * u + 2, lo:hi].rearrange("p t n -> p n t")
+            nc.scalar.copy(dst, src)
+
+        xq = {}
+        tg_w = {}
+        tg_s = {}
+
+        def gather_tab_scales(c):
+            tg_s[c] = kept("tg_s%d" % c, [P, CH], U8)
+            nc.vector.tensor_copy(tg_s[c][:], tab_sc[:].bitcast(U8).indirect(offs_sb[:, LCOL * c : LCOL * (c + 1)]))
+
+        def gather_tab_words(c):
+            tg_w[c] = kept("tg_w%d" % c, [P, CH], U32)
+            nc.vector.tensor_copy(tg_w[c][:], tab_w[:].bitcast(U32).indirect(offs_sb[:, LCOL * c : LCOL * (c + 1)]))
+
+        wt_p = kept("wt_p", [P, 2 * H], U8)
+        wt_sc = kept("wt_sc", [P, H], U8)
+
+        def permute_wt_words():
+            nc.vector.tensor_copy(
+                wt_p[:].bitcast(U16).rearrange("p (b t m) -> p b m t", b=2, t=PACK),
+                wt_raw[:].bitcast(U16).rearrange("p (b m t) -> p b m t", b=2, t=PACK),
+            )
+
+        def permute_wt_scales():
+            nc.vector.tensor_copy(
+                wt_sc[:].rearrange("p (b t m) -> p b m t", b=2, t=PACK),
+                wt_sc_raw[:].bitcast(U8).rearrange("p (b m t) -> p b m t", b=2, t=PACK),
+            )
+
+        hq = {}
+
+        biased, hb = {}, {}
+
+        def project_x(c, b, lo, hi):
+            if (c, b) not in biased:
+                biased[c, b] = ring.tile([P, PACK, CH], F32, name="f32x4", bufs=5)
+            for t in range(PACK):
+                acc = psum.tile([P, hi - lo], F32, name="acc", bufs=5)
+                for a in range(2):
+                    nc.tensor.matmul_mx(
+                        out=acc[:],
+                        lhsT=wq[a, b][0][:, P * t : P * (t + 1)].bitcast(FP8X4),
+                        lhsT_scale=wq[a, b][1][:, P * t : P * (t + 1)],
+                        rhs=xq[a, c][0][:, lo:hi].bitcast(FP8X4),
+                        rhs_scale=xq[a, c][1][:, lo:hi],
+                        start=(a == 0),
+                        stop=(a == 1),
+                    )
+                nc.scalar.activation(biased[c, b][:, t, lo:hi], acc[:], ACT.Identity, bias=bx_sb[:, b, t : t + 1])
+
+        def join(c, b, q):
+            if (c, b) not in hb:
+                hb[c, b] = ring.tile([P, CH * PACK], BF16, name="b16", bufs=7, align_bytes=64)
+            pb = psum.tile([P, PACK, P], F32, name="pb", bufs=3)
+            for t in range(PACK):
+                col = KP * b + P * t
+                nc.tensor.matmul_mx(
+                    out=pb[:, t, :],
+                    lhsT=wt_p[:, 2 * col : 2 * (col + P)].bitcast(FP4X4),
+                    lhsT_scale=wt_sc[:, col : col + P],
+                    rhs=tg_w[c][:, P * q : P * (q + 1)].bitcast(FP8X4),
+                    rhs_scale=tg_s[c][:, P * q : P * (q + 1)],
+                    start=True,
+                    stop=True,
+                )
+            nc.vector.tensor_tensor(
+                hb[c, b][:, PACK * P * q : PACK * P * (q + 1)].rearrange("p (c i t) -> p c t i", i=4, t=PACK),
+                pb[:].rearrange("p t (c i) -> p c t i", i=4),
+                biased[c, b][:, :, P * q : P * (q + 1)].rearrange("p t (c i) -> p c t i", i=4),
+                ALU.max,
+            )
+
+        def quantize_h(c, b, lo, hi):
+            if (c, b) not in hq:
+                hq[c, b] = kept("hq%d%d_c" % (c, b), [P, CH], U32), kept("hq%d%d_s" % (c, b), [P, CH], U8)
+            codes, scales = hq[c, b]
+            nc.vector.quantize_mx(
+                out=codes[:, lo:hi].bitcast(FP8X4), scales=scales[:, lo:hi], in_=hb[c, b][:, PACK * lo : PACK * hi]
+            )
+
+        def load_old(c):
+            old_sb[c] = ring.tile([P, N // P, CH], F32, name="plane", bufs=8)
+            nc.sync.dma_start(old_sb[c][:], old[:, CH * c : CH * (c + 1)].rearrange("(c p) j -> p c j", p=P))
+
+        def finish(c, lo, hi, adder, nts):
+            for nt in nts:
+                acc = psum.tile([P, hi - lo], F32, name="acc", bufs=5)
+                for b in range(2):
+                    nc.tensor.matmul_mx(
+                        out=acc[:],
+                        lhsT=wo_w[:, b, P * nt : P * (nt + 1)].bitcast(FP8X4),
+                        lhsT_scale=wo_sc[:, b, :].bitcast(U8)[:, P * nt : P * (nt + 1)],
+                        rhs=hq[c, b][0][:, lo:hi].bitcast(FP8X4),
+                        rhs_scale=hq[c, b][1][:, lo:hi],
+                        start=(b == 0),
+                        stop=(b == 1),
+                    )
+                th = ring.tile([P, hi - lo], F32, name="th", bufs=6)
+                nc.scalar.activation(th[:], acc[:], ACT.Tanh, bias=bo_sb[:, nt : nt + 1])
+                adder.tensor_tensor(old_sb[c][:, nt, lo:hi], old_sb[c][:, nt, lo:hi], th[:], ALU.add)
+                nc.sync.dma_start(out[P * nt : P * (nt + 1), CH * c + lo : CH * c + hi], old_sb[c][:, nt, lo:hi])
+
+        nc.sync.dma_start(wgt_sb[:, :CH], wgt[:, :CH])
+        nc.sync.dma_start(offs_sb[:], offs)
+        load_scale_rows(nc.sync, tab_sc, tab_scales[0])
+        nc.sync.dma_start(offs2_sb[:], offs2)
+        load_plane(0, 0)
+        load_wx(0, 0)
+        nc.sync.dma_start(wgt_sb[:, CH:], wgt[:, CH:])
+        nc.sync.dma_start(wt_raw[:], wt_words[0].bitcast(I32))
+        load_plane(0, 1)
+        load_scale_rows(nc.sync, wt_sc_raw, wt_scales[0])
+        load_plane(0, 2)
+        load_plane(0, 3)
+        load_plane(1, 1)
+        load_plane(1, 0)
+        load_wx(1, 0)
+        load_plane(1, 2)
+        load_plane(1, 3)
+        nc.sync.dma_start(tab_w[:], tab_words[0].rearrange("p t i -> p (t i)").bitcast(I32))
+        load_wx(0, 1)
+        load_wx(1, 1)
+        gather(0, 1, 1)
+        nc.sync.dma_start(bx_sb[:], bx.rearrange("(b p t) -> p b t", b=2, t=PACK))
+        gather(0, 1, 0)
+        gather(0, 0, 0)
+        nc.sync.dma_start(wo_w[:], wo_words.rearrange("a p n t -> p a (n t)").bitcast(I32))
+        gather(0, 2, 1)
+        with nc.allow_non_contiguous_dma(reason="one bias value to a partition"):
+            nc.sync.dma_start(bo_sb[:], bo.rearrange("(c p) -> p c", p=P))
+        gather_tab_scales(0)
+        gather_tab_scales(1)
+        gather(0, 0, 1)
+        gather(1, 2, 0)
+        load_old(0)
+        gather(0, 3, 0)
+        wb11 = cast_wx(1, 1, "scalar")
+        gather(1, 0, 0)
+        gather(0, 3, 1)
+        interleave(0, 1, 0, CH, "scalar")
+        load_old(1)
+        permute_wt_scales()
+        permute_wt_words()
+        wb00 = cast_wx(0, 0, "scalar")
+        gather(0, 2, 0)
+        interleave(0, 0, 0, CH, "scalar")
+        wb10 = cast_wx(1, 0, "scalar")
+        gather(1, 1, 0)
+        xq[0, 0] = quantize("xq00", xb[0, 0][:])
+        gather(1, 0, 1)
+        gather(1, 3, 0, 0, 256)
+        gather(1, 2, 1)
+        interleave_pair(1, 0, 0, 0, CH)
+        wq[0, 0] = quantize("wq00", wb00[:])
+        xq[0, 1] = quantize("xq01", xb[0, 1][:])
+        gather(1, 1, 1)
+        wq[1, 0] = quantize("wq10", wb10[:])
+        gather_tab_words(0)
+        interleave_pair(1, 0, 1, 0, 256)
+        interleave_pair(1, 1, 0, 0, CH)
+        gather(1, 3, 0, 256, 512)
+        gather(1, 3, 1, 0, 256)
+        interleave_pair(1, 1, 1, 0, 256)
+        gather(1, 3, 1, 256, 512)
+        interleave_pair(1, 0, 1, 256, 512)
+        xq[1, 0] = quantize("xq10", xb[1, 0][:])
+        project_x(0, 0, 0, 512)
+        join(0, 0, 1)
+        gather_tab_words(1)
+        wb01 = cast_wx(0, 1, "vector")
+        interleave_pair(1, 1, 1, 256, 512)
+        wq[0, 1] = quantize("wq01", wb01[:])
+        load_scale_rows(nc.sync, wo_sc, wo_scales.rearrange("a r n -> r a n"))
+        wq[1, 1] = quantize("wq11", wb11[:])
+        join(0, 0, 2)
+        join(0, 0, 0)
+        join(0, 0, 3)
+        xq[1, 1] = quantize("xq11", xb[1, 1][:])
+        project_x(1, 0, 0, 512)
+        join(1, 0, 2)
+        quantize_h(0, 0, 0, 512)
+        project_x(0, 1, 0, 512)
+        join(1, 0, 1)
+        join(1, 0, 0)
+        join(1, 0, 3)
+        quantize_h(1, 0, 0, 512)
+        join(0, 1, 2)
+        project_x(1, 1, 256, 512)
+        join(0, 1, 0)
+        join(0, 1, 3)
+        join(0, 1, 1)
+        project_x(1, 1, 0, 256)
+        join(1, 1, 0)
+        quantize_h(0, 1, 0, 512)
+        join(1, 1, 3)
+        join(1, 1, 2)
+        join(1, 1, 1)
+        quantize_h(1, 1, 0, 256)
+        finish(1, 0, 256, nc.vector, [0])
+        quantize_h(1, 1, 256, 512)
+        finish(1, 0, 256, nc.vector, [3])
+        finish(0, 0, 512, nc.vector, [3])
+        finish(0, 0, 512, nc.vector, [0])
+        finish(0, 0, 512, nc.vector, [2])
+        finish(1, 256, 512, nc.vector, [0])
+        finish(1, 0, 256, nc.vector, [1])
+        finish(1, 0, 256, nc.vector, [2])
+        finish(0, 0, 512, nc.vector, [1])
+        finish(1, 256, 512, nc.vector, [2])
+        finish(1, 256, 512, nc.vector, [1])
+        finish(1, 256, 512, nc.vector, [3])

@@ -54,8 +54,8 @@ def tile_list_relation_type_max_kernel(
         bo_sb = kept("bo_sb", [P, N // P], F32)
 
         def load_scale_rows(queue, tile, rows):
-            for q in range(4):
-                queue.dma_start(tile[32 * q : 32 * q + 4], rows[4 * q : 4 * q + 4].bitcast(I32))
+            for r in range(4):
+                queue.dma_start(tile[r:P:32], rows[r:16:4].bitcast(I32))
 
         wt_raw = kept("wt_raw", [P, H // 2], I32)
         wgt_sb = kept("wgt_sb", [P, S], F32)
@@ -125,16 +125,14 @@ def tile_list_relation_type_max_kernel(
             nc.scalar.copy(dst, src)
 
         xq = {}
-        tg_w = {}
-        tg_s = {}
+        tg_s = kept("tg_s", [P, S], U8)
+        tg_w = kept("tg_w", [P, S], U32)
 
-        def gather_tab_scales(c):
-            tg_s[c] = kept("tg_s%d" % c, [P, CH], U8)
-            nc.vector.tensor_copy(tg_s[c][:], tab_sc[:].bitcast(U8).indirect(offs_sb[:, LCOL * c : LCOL * (c + 1)]))
+        def gather_tab_scales(lo, hi):
+            nc.vector.tensor_copy(tg_s[:, lo:hi], tab_sc[:].bitcast(U8).indirect(offs_sb[:, lo // 16 : hi // 16]))
 
-        def gather_tab_words(c):
-            tg_w[c] = kept("tg_w%d" % c, [P, CH], U32)
-            nc.vector.tensor_copy(tg_w[c][:], tab_w[:].bitcast(U32).indirect(offs_sb[:, LCOL * c : LCOL * (c + 1)]))
+        def gather_tab_words(lo, hi):
+            nc.vector.tensor_copy(tg_w[:, lo:hi], tab_w[:].bitcast(U32).indirect(offs_sb[:, lo // 16 : hi // 16]))
 
         wt_p = kept("wt_p", [P, 2 * H], U8)
         wt_sc = kept("wt_sc", [P, H], U8)
@@ -182,8 +180,8 @@ def tile_list_relation_type_max_kernel(
                     out=pb[:, t, :],
                     lhsT=wt_p[:, 2 * col : 2 * (col + P)].bitcast(FP4X4),
                     lhsT_scale=wt_sc[:, col : col + P],
-                    rhs=tg_w[c][:, P * q : P * (q + 1)].bitcast(FP8X4),
-                    rhs_scale=tg_s[c][:, P * q : P * (q + 1)],
+                    rhs=tg_w[:, CH * c + P * q : CH * c + P * (q + 1)].bitcast(FP8X4),
+                    rhs_scale=tg_s[:, CH * c + P * q : CH * c + P * (q + 1)],
                     start=True,
                     stop=True,
                 )
@@ -224,112 +222,104 @@ def tile_list_relation_type_max_kernel(
                 adder.tensor_tensor(old_sb[c][:, nt, lo:hi], old_sb[c][:, nt, lo:hi], th[:], ALU.add)
                 nc.sync.dma_start(out[P * nt : P * (nt + 1), CH * c + lo : CH * c + hi], old_sb[c][:, nt, lo:hi])
 
-        nc.sync.dma_start(wgt_sb[:, :CH], wgt[:, :CH])
+        nc.sync.dma_start(wt_raw[:], wt_words[0].bitcast(I32))
         nc.sync.dma_start(offs_sb[:], offs)
         load_scale_rows(nc.sync, tab_sc, tab_scales[0])
         nc.sync.dma_start(offs2_sb[:], offs2)
         load_plane(0, 0)
-        load_wx(0, 0)
-        nc.sync.dma_start(wgt_sb[:, CH:], wgt[:, CH:])
-        nc.sync.dma_start(wt_raw[:], wt_words[0].bitcast(I32))
-        load_plane(0, 1)
         load_scale_rows(nc.sync, wt_sc_raw, wt_scales[0])
+        nc.sync.dma_start(wgt_sb[:], wgt)
+        load_plane(0, 1)
         load_plane(0, 2)
         load_plane(0, 3)
-        load_plane(1, 1)
         load_plane(1, 0)
+        load_plane(1, 1)
+        load_wx(0, 0)
         load_wx(1, 0)
         load_plane(1, 2)
         load_plane(1, 3)
         nc.sync.dma_start(tab_w[:], tab_words[0].rearrange("p t i -> p (t i)").bitcast(I32))
         load_wx(0, 1)
         load_wx(1, 1)
-        gather(0, 1, 1)
+        load_scale_rows(nc.sync, wo_sc, wo_scales.rearrange("a r n -> r a n"))
         nc.sync.dma_start(bx_sb[:], bx.rearrange("(b p t) -> p b t", b=2, t=PACK))
-        gather(0, 1, 0)
-        gather(0, 0, 0)
-        nc.sync.dma_start(wo_w[:], wo_words.rearrange("a p n t -> p a (n t)").bitcast(I32))
-        gather(0, 2, 1)
-        with nc.allow_non_contiguous_dma(reason="one bias value to a partition"):
-            nc.sync.dma_start(bo_sb[:], bo.rearrange("(c p) -> p c", p=P))
-        gather_tab_scales(0)
-        gather_tab_scales(1)
-        gather(0, 0, 1)
-        gather(1, 2, 0)
-        load_old(0)
-        gather(0, 3, 0)
-        wb11 = cast_wx(1, 1, "scalar")
-        gather(1, 0, 0)
-        gather(0, 3, 1)
-        interleave(0, 1, 0, CH, "scalar")
-        load_old(1)
+        gather_tab_scales(0, S)
         permute_wt_scales()
         permute_wt_words()
-        wb00 = cast_wx(0, 0, "scalar")
+        gather(0, 0, 0)
+        gather(0, 0, 1)
+        gather(0, 1, 0)
+        gather(0, 1, 1)
+        load_old(0)
+        load_old(1)
+        with nc.allow_non_contiguous_dma(reason="one bias value to a partition"):
+            nc.sync.dma_start(bo_sb[:], bo.rearrange("(c p) -> p c", p=P))
+        nc.sync.dma_start(wo_w[:], wo_words.rearrange("a p n t -> p a (n t)").bitcast(I32))
+        interleave_pair(0, 0, 0, 0, CH)
+        interleave_pair(0, 1, 0, 0, CH)
         gather(0, 2, 0)
-        interleave(0, 0, 0, CH, "scalar")
-        wb10 = cast_wx(1, 0, "scalar")
-        gather(1, 1, 0)
-        xq[0, 0] = quantize("xq00", xb[0, 0][:])
+        gather(0, 2, 1)
+        gather(0, 3, 0)
+        gather(0, 3, 1)
+        interleave_pair(0, 0, 1, 0, CH)
+        interleave_pair(0, 1, 1, 0, CH)
+        gather(1, 0, 0)
         gather(1, 0, 1)
-        gather(1, 3, 0, 0, 256)
-        gather(1, 2, 1)
-        interleave_pair(1, 0, 0, 0, CH)
-        wq[0, 0] = quantize("wq00", wb00[:])
-        xq[0, 1] = quantize("xq01", xb[0, 1][:])
+        gather(1, 1, 0)
         gather(1, 1, 1)
-        wq[1, 0] = quantize("wq10", wb10[:])
-        gather_tab_words(0)
-        interleave_pair(1, 0, 1, 0, 256)
+        wb00 = cast_wx(0, 0, "scalar")
+        wb10 = cast_wx(1, 0, "scalar")
+        interleave_pair(1, 0, 0, 0, CH)
         interleave_pair(1, 1, 0, 0, CH)
+        gather(1, 2, 0)
+        gather(1, 2, 1)
+        xq[0, 0] = quantize("xq00", xb[0, 0][:])
+        xq[0, 1] = quantize("xq01", xb[0, 1][:])
+        wq[0, 0] = quantize("wq00", wb00[:])
+        wq[1, 0] = quantize("wq10", wb10[:])
+        gather(1, 3, 0, 0, 256)
+        interleave_pair(1, 0, 1, 0, 256)
         gather(1, 3, 0, 256, 512)
-        gather(1, 3, 1, 0, 256)
-        interleave_pair(1, 1, 1, 0, 256)
-        gather(1, 3, 1, 256, 512)
         interleave_pair(1, 0, 1, 256, 512)
-        xq[1, 0] = quantize("xq10", xb[1, 0][:])
-        project_x(0, 0, 0, 512)
-        join(0, 0, 1)
-        gather_tab_words(1)
-        wb01 = cast_wx(0, 1, "vector")
+        gather(1, 3, 1)
+        interleave_pair(1, 1, 1, 0, 256)
         interleave_pair(1, 1, 1, 256, 512)
-        wq[0, 1] = quantize("wq01", wb01[:])
-        load_scale_rows(nc.sync, wo_sc, wo_scales.rearrange("a r n -> r a n"))
-        wq[1, 1] = quantize("wq11", wb11[:])
-        join(0, 0, 2)
-        join(0, 0, 0)
-        join(0, 0, 3)
+        gather_tab_words(0, S)
+        xq[1, 0] = quantize("xq10", xb[1, 0][:])
         xq[1, 1] = quantize("xq11", xb[1, 1][:])
+        wb11 = cast_wx(1, 1, "vector")
+        wb01 = cast_wx(0, 1, "scalar")
+        wq[0, 1] = quantize("wq01", wb01[:])
+        wq[1, 1] = quantize("wq11", wb11[:])
+        project_x(0, 0, 0, 512)
+        join(0, 0, 0)
+        join(0, 0, 1)
+        join(0, 0, 2)
+        join(0, 0, 3)
         project_x(1, 0, 0, 512)
-        join(1, 0, 2)
-        quantize_h(0, 0, 0, 512)
-        project_x(0, 1, 0, 512)
-        join(1, 0, 1)
         join(1, 0, 0)
+        join(1, 0, 1)
+        join(1, 0, 2)
         join(1, 0, 3)
-        quantize_h(1, 0, 0, 512)
-        join(0, 1, 2)
-        project_x(1, 1, 256, 512)
+        project_x(0, 1, 0, 512)
         join(0, 1, 0)
-        join(0, 1, 3)
         join(0, 1, 1)
-        project_x(1, 1, 0, 256)
-        join(1, 1, 0)
+        join(0, 1, 2)
+        join(0, 1, 3)
+        project_x(1, 1, 0, 512)
+        quantize_h(0, 0, 0, 512)
         quantize_h(0, 1, 0, 512)
-        join(1, 1, 3)
-        join(1, 1, 2)
+        quantize_h(1, 0, 0, 512)
+        join(1, 1, 0)
         join(1, 1, 1)
-        quantize_h(1, 1, 0, 256)
-        finish(1, 0, 256, nc.vector, [0])
-        quantize_h(1, 1, 256, 512)
-        finish(1, 0, 256, nc.vector, [3])
-        finish(0, 0, 512, nc.vector, [3])
+        join(1, 1, 2)
+        join(1, 1, 3)
+        quantize_h(1, 1, 0, 512)
         finish(0, 0, 512, nc.vector, [0])
-        finish(0, 0, 512, nc.vector, [2])
-        finish(1, 256, 512, nc.vector, [0])
-        finish(1, 0, 256, nc.vector, [1])
-        finish(1, 0, 256, nc.vector, [2])
         finish(0, 0, 512, nc.vector, [1])
-        finish(1, 256, 512, nc.vector, [2])
-        finish(1, 256, 512, nc.vector, [1])
-        finish(1, 256, 512, nc.vector, [3])
+        finish(0, 0, 512, nc.vector, [2])
+        finish(0, 0, 512, nc.vector, [3])
+        finish(1, 0, 512, nc.vector, [0])
+        finish(1, 0, 512, nc.vector, [1])
+        finish(1, 0, 512, nc.vector, [2])
+        finish(1, 0, 512, nc.vector, [3])

@@ -46,10 +46,6 @@ def tile_list_relation_type_max_kernel(
         nc.vector.memset(tab_sc[:], 0)
         nc.vector.memset(wt_sc_raw[:], 0)
         nc.vector.memset(wo_sc[:], 0)
-        warm = kept("warm", [P, 1], F32)
-        nc.vector.memset(warm[:], 0.0)
-        warm_out = kept("warm_out", [P, 1], F32)
-        nc.scalar.activation(warm_out[:], warm[:], ACT.Tanh)
         bx_sb = kept("bx_sb", [P, 2, PACK], F32)
         bo_sb = kept("bo_sb", [P, N // P], F32)
 

@@ -21,7 +21,6 @@ PACK = 4
 KP = P * PACK
 CH = 512
 NCH = S // CH
-LCOL = CH // 16
 
 
 def tile_list_relation_type_max_kernel(
@@ -33,9 +32,13 @@ def tile_list_relation_type_max_kernel(
         keep = ctx.enter_context(tc.tile_pool(name="keep", bufs=1))
         ring = ctx.enter_context(tc.tile_pool(name="ring", bufs=2))
         psum = ctx.enter_context(tc.psum_pool(name="psum", bufs=1))
+        bufs = {"plane": 6, "wx_raw": 3, "b16": 8, "codes": 11, "pair": 4, "f32x4": 4, "th": 6, "acc": 5, "pb": 3}
 
         def kept(name, shape, dtype):
             return keep.tile(shape, dtype, name=name, align_bytes=64)
+
+        def tagged(tag, shape, dtype):
+            return ring.tile(shape, dtype, name=tag, bufs=bufs[tag], align_bytes=64)
 
         offs2_sb = lists.tile([P, S // 16], U16, name="offs2_sb")
         offs_sb = lists.tile([P, S // 16], U16, name="offs_sb")
@@ -49,86 +52,84 @@ def tile_list_relation_type_max_kernel(
         bx_sb = kept("bx_sb", [P, 2, PACK], F32)
         bo_sb = kept("bo_sb", [P, N // P], F32)
 
-        def load_scale_rows(queue, tile, rows):
+        def load_scale_rows(tile, rows):
             for r in range(4):
-                queue.dma_start(tile[r:P:32], rows[r:16:4].bitcast(I32))
+                nc.sync.dma_start(tile[r:P:32], rows[r:16:4].bitcast(I32))
 
         wt_raw = kept("wt_raw", [P, H // 2], I32)
         wgt_sb = kept("wgt_sb", [P, S], F32)
         tab_w = kept("tab_w", [P, V], I32)
         wo_w = kept("wo_w", [P, 2, N], I32)
-        old_sb = {}
-        planes = {}
-        wx_raw = {}
+        old_sb, planes, wx_raw = {}, {}, {}
 
         def load_plane(a, i):
-            planes[a, i] = ring.tile([P, T], F32, name="plane", bufs=8)
+            planes[a, i] = tagged("plane", [P, T], F32)
             rows = xT[KP * a : KP * (a + 1), :].rearrange("(p i) t -> p i t", i=PACK)
             nc.sync.dma_start(planes[a, i][:], rows[:, i, :])
 
         def load_wx(a, b):
-            wx_raw[a, b] = ring.tile([P, PACK, KP], F32, name="wx_raw", bufs=4)
+            wx_raw[a, b] = tagged("wx_raw", [P, PACK, KP], F32)
             rows = wx[KP * a : KP * (a + 1), KP * b : KP * (b + 1)].rearrange("(p j) c -> p j c", j=PACK)
             nc.sync.dma_start(wx_raw[a, b][:], rows)
 
-        wq = {}
+        def load_old(c):
+            old_sb[c] = tagged("plane", [P, N // P, CH], F32)
+            nc.sync.dma_start(old_sb[c][:], old[:, CH * c : CH * (c + 1)].rearrange("(c p) j -> p c j", p=P))
 
-        def cast_wx(a, b, engine):
-            wb = ring.tile([P, KP * PACK], BF16, name="b16", bufs=7, align_bytes=64)
-            dst = wb[:].rearrange("p (t m j) -> p m j t", t=PACK, j=PACK)
-            src = wx_raw[a, b][:].rearrange("p j (m t) -> p m j t", t=PACK)
-            if engine == "scalar":
-                nc.scalar.copy(dst, src)
-            else:
-                nc.vector.tensor_copy(dst, src)
-            return wb
+        wb, wq, xb, xq, g, tg_w = {}, {}, {}, {}, {}, {}
 
-        def quantize(name, src):
-            codes = kept(name + "_c", [P, src.shape[1] // PACK], U32)
-            scales = kept(name + "_s", [P, src.shape[1] // PACK], U8)
-            nc.vector.quantize_mx(out=codes[:].bitcast(FP8X4), scales=scales[:], in_=src)
+        def cast_wx(a, b, copy):
+            wb[a, b] = tagged("b16", [P, KP * PACK], BF16)
+            copy(
+                wb[a, b][:].rearrange("p (t m j) -> p m j t", t=PACK, j=PACK),
+                wx_raw[a, b][:].rearrange("p j (m t) -> p m j t", t=PACK),
+            )
+
+        def quantize(name, src, tag):
+            codes = tagged(tag, [P, CH], U32)
+            scales = kept(name + "_s", [P, CH], U8)
+            nc.vector.quantize_mx(out=codes[:].bitcast(FP8X4), scales=scales[:], in_=src[:])
             return codes, scales
 
-        g = {}
+        def new_quad(a, c):
+            quad = tagged("f32x4", [P, PACK, CH], F32)
+            g[a, c] = quad
+            for i in range(PACK):
+                g[a, c, i] = quad[:, i, :]
+
+        def new_pair(a, c, u):
+            pair = tagged("pair", [P, 2, CH], F32)
+            g[a, c, "pair", u] = pair
+            for e in range(2):
+                g[a, c, 2 * u + e] = pair[:, e, :]
 
         def gather(a, i, c, lo=0, hi=CH):
-            if (a, c) not in g:
-                g[a, c] = ring.tile([P, PACK, CH], F32, name="f32x4", bufs=5)
             nc.vector.tensor_tensor(
-                g[a, c][:, i, lo:hi],
+                g[a, c, i][:, lo:hi],
                 planes[a, i][:].indirect(offs2_sb[:, (CH * c + lo) // 16 : (CH * c + hi) // 16]),
                 wgt_sb[:, CH * c + lo : CH * c + hi],
                 ALU.mult,
             )
 
-        xb = {}
-
-        def interleave(a, c, lo, hi, engine):
-            if (a, c) not in xb:
-                xb[a, c] = ring.tile([P, CH * PACK], BF16, name="b16", bufs=7, align_bytes=64)
-            dst = xb[a, c][:, PACK * lo : PACK * hi].rearrange("p (c i t) -> p c t i", i=4, t=PACK)
-            src = g[a, c][:, :, lo:hi].rearrange("p t (c i) -> p c t i", i=4)
-            if engine == "scalar":
-                nc.scalar.copy(dst, src)
-            else:
-                nc.vector.tensor_copy(dst, src)
+        def interleave(a, c):
+            xb[a, c] = tagged("b16", [P, CH * PACK], BF16)
+            nc.scalar.copy(
+                xb[a, c][:].rearrange("p (c i t) -> p c t i", i=4, t=PACK),
+                g[a, c][:].rearrange("p t (c i) -> p c t i", i=4),
+            )
 
         def interleave_pair(a, c, u, lo, hi):
             if (a, c) not in xb:
-                xb[a, c] = ring.tile([P, CH * PACK], BF16, name="b16", bufs=7, align_bytes=64)
+                xb[a, c] = tagged("b16", [P, CH * PACK], BF16)
             dst = xb[a, c][:, PACK * lo : PACK * hi].rearrange("p (n t) -> p n t", t=PACK)[:, :, 2 * u : 2 * u + 2]
-            src = g[a, c][:, 2 * u : 2 * u + 2, lo:hi].rearrange("p t n -> p n t")
-            nc.scalar.copy(dst, src)
+            nc.scalar.copy(dst, g[a, c, "pair", u][:, :, lo:hi].rearrange("p t n -> p n t"))
 
-        xq = {}
         tg_s = kept("tg_s", [P, S], U8)
-        tg_w = kept("tg_w", [P, S], U32)
 
-        def gather_tab_scales(lo, hi):
-            nc.vector.tensor_copy(tg_s[:, lo:hi], tab_sc[:].bitcast(U8).indirect(offs_sb[:, lo // 16 : hi // 16]))
-
-        def gather_tab_words(lo, hi):
-            nc.vector.tensor_copy(tg_w[:, lo:hi], tab_w[:].bitcast(U32).indirect(offs_sb[:, lo // 16 : hi // 16]))
+        def gather_tab_words(c, tag):
+            tg_w[c] = tagged(tag, [P, CH], U32)
+            cols = slice(CH * c // 16, CH * (c + 1) // 16)
+            nc.vector.tensor_copy(tg_w[c][:], tab_w[:].bitcast(U32).indirect(offs_sb[:, cols]))
 
         wt_p = kept("wt_p", [P, 2 * H], U8)
         wt_sc = kept("wt_sc", [P, H], U8)
@@ -145,15 +146,13 @@ def tile_list_relation_type_max_kernel(
                 wt_sc_raw[:].bitcast(U8).rearrange("p (b m t) -> p b m t", b=2, t=PACK),
             )
 
-        hq = {}
+        hq, biased, hb = {}, {}, {}
 
-        biased, hb = {}, {}
-
-        def project_x(c, b, lo, hi):
+        def project_x(c, b, lo=0, hi=CH):
             if (c, b) not in biased:
-                biased[c, b] = ring.tile([P, PACK, CH], F32, name="f32x4", bufs=5)
+                biased[c, b] = tagged("f32x4", [P, PACK, CH], F32)
             for t in range(PACK):
-                acc = psum.tile([P, hi - lo], F32, name="acc", bufs=5)
+                acc = psum.tile([P, hi - lo], F32, name="acc", bufs=bufs["acc"])
                 for a in range(2):
                     nc.tensor.matmul_mx(
                         out=acc[:],
@@ -168,15 +167,15 @@ def tile_list_relation_type_max_kernel(
 
         def join(c, b, q):
             if (c, b) not in hb:
-                hb[c, b] = ring.tile([P, CH * PACK], BF16, name="b16", bufs=7, align_bytes=64)
-            pb = psum.tile([P, PACK, P], F32, name="pb", bufs=3)
+                hb[c, b] = tagged("b16", [P, CH * PACK], BF16)
+            pb = psum.tile([P, PACK, P], F32, name="pb", bufs=bufs["pb"])
             for t in range(PACK):
                 col = KP * b + P * t
                 nc.tensor.matmul_mx(
                     out=pb[:, t, :],
                     lhsT=wt_p[:, 2 * col : 2 * (col + P)].bitcast(FP4X4),
                     lhsT_scale=wt_sc[:, col : col + P],
-                    rhs=tg_w[:, CH * c + P * q : CH * c + P * (q + 1)].bitcast(FP8X4),
+                    rhs=tg_w[c][:, P * q : P * (q + 1)].bitcast(FP8X4),
                     rhs_scale=tg_s[:, CH * c + P * q : CH * c + P * (q + 1)],
                     start=True,
                     stop=True,
@@ -188,21 +187,20 @@ def tile_list_relation_type_max_kernel(
                 ALU.max,
             )
 
-        def quantize_h(c, b, lo, hi):
+        def quantize_h(c, b, tag, lo=0, hi=CH):
             if (c, b) not in hq:
-                hq[c, b] = kept("hq%d%d_c" % (c, b), [P, CH], U32), kept("hq%d%d_s" % (c, b), [P, CH], U8)
+                hq[c, b] = tagged(tag, [P, CH], U32), kept("hq%d%d_s" % (c, b), [P, CH], U8)
             codes, scales = hq[c, b]
             nc.vector.quantize_mx(
                 out=codes[:, lo:hi].bitcast(FP8X4), scales=scales[:, lo:hi], in_=hb[c, b][:, PACK * lo : PACK * hi]
             )
 
-        def load_old(c):
-            old_sb[c] = ring.tile([P, N // P, CH], F32, name="plane", bufs=8)
-            nc.sync.dma_start(old_sb[c][:], old[:, CH * c : CH * (c + 1)].rearrange("(c p) j -> p c j", p=P))
+        th = {}
 
-        def finish(c, lo, hi, adder, nts):
-            for nt in nts:
-                acc = psum.tile([P, hi - lo], F32, name="acc", bufs=5)
+        def project_h(c, lo, hi, nts):
+            th[c, lo, nts[0]] = tagged("th", [P, len(nts), hi - lo], F32)
+            for k, nt in enumerate(nts):
+                acc = psum.tile([P, hi - lo], F32, name="acc", bufs=bufs["acc"])
                 for b in range(2):
                     nc.tensor.matmul_mx(
                         out=acc[:],
@@ -213,109 +211,92 @@ def tile_list_relation_type_max_kernel(
                         start=(b == 0),
                         stop=(b == 1),
                     )
-                th = ring.tile([P, hi - lo], F32, name="th", bufs=6)
-                nc.scalar.activation(th[:], acc[:], ACT.Tanh, bias=bo_sb[:, nt : nt + 1])
-                adder.tensor_tensor(old_sb[c][:, nt, lo:hi], old_sb[c][:, nt, lo:hi], th[:], ALU.add)
-                nc.sync.dma_start(out[P * nt : P * (nt + 1), CH * c + lo : CH * c + hi], old_sb[c][:, nt, lo:hi])
+                nc.scalar.activation(th[c, lo, nts[0]][:, k, :], acc[:], ACT.Tanh, bias=bo_sb[:, nt : nt + 1])
+
+        def update(c, lo, hi, nts, adder):
+            rows = old_sb[c][:, nts[0] : nts[-1] + 1, lo:hi]
+            adder.tensor_tensor(rows, rows, th[c, lo, nts[0]][:], ALU.add)
+            dst = out[P * nts[0] : P * (nts[-1] + 1), CH * c + lo : CH * c + hi].rearrange("(c p) j -> p c j", p=P)
+            nc.sync.dma_start(dst, rows)
 
         nc.sync.dma_start(wt_raw[:], wt_words[0].bitcast(I32))
         nc.sync.dma_start(offs_sb[:], offs)
-        load_scale_rows(nc.sync, tab_sc, tab_scales[0])
+        load_scale_rows(tab_sc, tab_scales[0])
         nc.sync.dma_start(offs2_sb[:], offs2)
         load_plane(0, 0)
-        load_scale_rows(nc.sync, wt_sc_raw, wt_scales[0])
+        load_scale_rows(wt_sc_raw, wt_scales[0])
         nc.sync.dma_start(wgt_sb[:], wgt)
         load_plane(0, 1)
         load_plane(0, 2)
         load_plane(0, 3)
+        load_wx(0, 0)
         load_plane(1, 0)
         load_plane(1, 1)
-        load_wx(0, 0)
         load_wx(1, 0)
         load_plane(1, 2)
-        load_plane(1, 3)
-        nc.sync.dma_start(tab_w[:], tab_words[0].rearrange("p t i -> p (t i)").bitcast(I32))
         load_wx(0, 1)
-        load_wx(1, 1)
-        load_scale_rows(nc.sync, wo_sc, wo_scales.rearrange("a r n -> r a n"))
+        load_plane(1, 3)
         nc.sync.dma_start(bx_sb[:], bx.rearrange("(b p t) -> p b t", b=2, t=PACK))
-        gather_tab_scales(0, S)
-        permute_wt_scales()
-        permute_wt_words()
-        gather(0, 0, 0)
-        gather(0, 0, 1)
-        gather(0, 1, 0)
-        gather(0, 1, 1)
-        load_old(0)
-        load_old(1)
+        nc.sync.dma_start(tab_w[:], tab_words[0].rearrange("p t i -> p (t i)").bitcast(I32))
+        load_wx(1, 1)
+        load_scale_rows(wo_sc, wo_scales.rearrange("a r n -> r a n"))
+        nc.sync.dma_start(wo_w[:], wo_words.rearrange("a p n t -> p a (n t)").bitcast(I32))
         with nc.allow_non_contiguous_dma(reason="one bias value to a partition"):
             nc.sync.dma_start(bo_sb[:], bo.rearrange("(c p) -> p c", p=P))
-        nc.sync.dma_start(wo_w[:], wo_words.rearrange("a p n t -> p a (n t)").bitcast(I32))
-        interleave_pair(0, 0, 0, 0, CH)
-        interleave_pair(0, 1, 0, 0, CH)
-        gather(0, 2, 0)
-        gather(0, 2, 1)
-        gather(0, 3, 0)
-        gather(0, 3, 1)
-        interleave_pair(0, 0, 1, 0, CH)
-        interleave_pair(0, 1, 1, 0, CH)
+        nc.vector.tensor_copy(tg_s[:], tab_sc[:].bitcast(U8).indirect(offs_sb[:]))
+        permute_wt_scales()
+        permute_wt_words()
+        new_quad(0, 0)
+        new_quad(0, 1)
+        for i in range(PACK):
+            gather(0, i, 0)
+            gather(0, i, 1)
+        load_old(0)
+        load_old(1)
+        cast_wx(0, 0, nc.scalar.copy)
+        interleave(0, 0)
+        interleave(0, 1)
+        new_pair(1, 0, 0)
+        new_quad(1, 1)
         gather(1, 0, 0)
         gather(1, 0, 1)
+        wq[0, 0] = quantize("wq00", wb[0, 0], "pair")
+        xq[0, 0] = quantize("xq00", xb[0, 0], "codes")
         gather(1, 1, 0)
         gather(1, 1, 1)
-        wb00 = cast_wx(0, 0, "scalar")
-        wb10 = cast_wx(1, 0, "scalar")
+        xq[0, 1] = quantize("xq01", xb[0, 1], "codes")
         interleave_pair(1, 0, 0, 0, CH)
-        interleave_pair(1, 1, 0, 0, CH)
+        cast_wx(1, 0, nc.scalar.copy)
+        new_pair(1, 0, 1)
         gather(1, 2, 0)
         gather(1, 2, 1)
-        xq[0, 0] = quantize("xq00", xb[0, 0][:])
-        xq[0, 1] = quantize("xq01", xb[0, 1][:])
-        wq[0, 0] = quantize("wq00", wb00[:])
-        wq[1, 0] = quantize("wq10", wb10[:])
+        wq[1, 0] = quantize("wq10", wb[1, 0], "pair")
+        cast_wx(0, 1, nc.scalar.copy)
         gather(1, 3, 0, 0, 256)
         interleave_pair(1, 0, 1, 0, 256)
         gather(1, 3, 0, 256, 512)
         interleave_pair(1, 0, 1, 256, 512)
         gather(1, 3, 1)
-        interleave_pair(1, 1, 1, 0, 256)
-        interleave_pair(1, 1, 1, 256, 512)
-        gather_tab_words(0, S)
-        xq[1, 0] = quantize("xq10", xb[1, 0][:])
-        xq[1, 1] = quantize("xq11", xb[1, 1][:])
-        wb11 = cast_wx(1, 1, "vector")
-        wb01 = cast_wx(0, 1, "scalar")
-        wq[0, 1] = quantize("wq01", wb01[:])
-        wq[1, 1] = quantize("wq11", wb11[:])
-        project_x(0, 0, 0, 512)
-        join(0, 0, 0)
-        join(0, 0, 1)
-        join(0, 0, 2)
-        join(0, 0, 3)
-        project_x(1, 0, 0, 512)
-        join(1, 0, 0)
-        join(1, 0, 1)
-        join(1, 0, 2)
-        join(1, 0, 3)
-        project_x(0, 1, 0, 512)
-        join(0, 1, 0)
-        join(0, 1, 1)
-        join(0, 1, 2)
-        join(0, 1, 3)
-        project_x(1, 1, 0, 512)
-        quantize_h(0, 0, 0, 512)
-        quantize_h(0, 1, 0, 512)
-        quantize_h(1, 0, 0, 512)
-        join(1, 1, 0)
-        join(1, 1, 1)
-        join(1, 1, 2)
-        join(1, 1, 3)
-        quantize_h(1, 1, 0, 512)
-        finish(0, 0, 512, nc.vector, [0])
-        finish(0, 0, 512, nc.vector, [1])
-        finish(0, 0, 512, nc.vector, [2])
-        finish(0, 0, 512, nc.vector, [3])
-        finish(1, 0, 512, nc.vector, [0])
-        finish(1, 0, 512, nc.vector, [1])
-        finish(1, 0, 512, nc.vector, [2])
-        finish(1, 0, 512, nc.vector, [3])
+        xq[1, 0] = quantize("xq10", xb[1, 0], "codes")
+        wq[0, 1] = quantize("wq01", wb[0, 1], "codes")
+        interleave(1, 1)
+        gather_tab_words(0, "codes")
+        xq[1, 1] = quantize("xq11", xb[1, 1], "codes")
+        cast_wx(1, 1, nc.vector.tensor_copy)
+        gather_tab_words(1, "b16")
+        wq[1, 1] = quantize("wq11", wb[1, 1], "codes")
+        for c, b in ((0, 0), (1, 0), (0, 1)):
+            project_x(c, b)
+            for q in range(4):
+                join(c, b, q)
+        project_x(1, 1)
+        quantize_h(0, 0, "codes")
+        quantize_h(0, 1, "codes")
+        for q in range(4):
+            join(1, 1, q)
+        quantize_h(1, 0, "codes")
+        quantize_h(1, 1, "codes")
+        for c in range(NCH):
+            for nt in range(4):
+                project_h(c, 0, CH, [nt])
+                update(c, 0, CH, [nt], nc.vector)

@@ -1,6 +1,7 @@
 from contextlib import ExitStack
 
 import concourse.mybir as mybir
+from concourse.masks import make_identity
 
 K, D, H, N, T, V, S = 1024, 512, 1024, 512, 2048, 2048, 1024
 FLOPS = 2 * S * (K * H + D * H + H * N)
@@ -21,6 +22,8 @@ PACK = 4
 KP = P * PACK
 CH = 512
 NCH = S // CH
+R, GROUP = 8, 16
+NB = S // P
 
 
 def tile_list_relation_type_max_kernel(
@@ -32,7 +35,7 @@ def tile_list_relation_type_max_kernel(
         keep = ctx.enter_context(tc.tile_pool(name="keep", bufs=1))
         ring = ctx.enter_context(tc.tile_pool(name="ring", bufs=2))
         psum = ctx.enter_context(tc.psum_pool(name="psum", bufs=1))
-        bufs = {"plane": 6, "wx_raw": 3, "b16": 8, "codes": 11, "pair": 4, "f32x4": 4, "th": 6, "acc": 5, "pb": 3}
+        bufs = {"plane": 5, "wx_raw": 3, "b16": 8, "tgs": 2, "codes": 12, "pair": 4, "f32x4": 4, "p_sb": 4, "th": 5, "acc": 8}
 
         def kept(name, shape, dtype):
             return keep.tile(shape, dtype, name=name, align_bytes=64)
@@ -58,9 +61,29 @@ def tile_list_relation_type_max_kernel(
 
         wt_raw = kept("wt_raw", [P, H // 2], I32)
         wgt_sb = kept("wgt_sb", [P, S], F32)
-        tab_w = kept("tab_w", [P, V], I32)
+        tab_w = tagged("plane", [P, V], I32)
         wo_w = kept("wo_w", [P, 2, N], I32)
         old_sb, planes, wx_raw = {}, {}, {}
+
+        w_rows = kept("w_rows", [P, P], F32)
+        ident = kept("ident", [P, P], F32)
+
+        def load_edge_weights():
+            nc.gpsimd.memset(w_rows[R * NB : P, :], 0.0)
+            make_identity(nc, ident[:])
+            nc.sync.dma_start(w_rows[0 : R * NB, :], wgt[0:P:GROUP, :].rearrange("g (b j) -> g b j", j=P))
+
+        def spread_edge_weights():
+            turned = psum.tile([P, P], F32, name="acc", bufs=bufs["acc"])
+            nc.tensor.transpose(turned[:], w_rows[:], ident[:])
+            by_block = turned[:, 0 : R * NB].rearrange("j (g b) -> j b g", b=NB)
+            for c in range(NCH):
+                wide = tagged("pair", [P, PACK, R, GROUP], F32)
+                nc.scalar.copy(wide[:], by_block[:, PACK * c : PACK * (c + 1), :].unsqueeze(3).to_broadcast([P, PACK, R, GROUP]))
+                back = psum.tile([P, PACK, P], F32, name="acc", bufs=bufs["acc"])
+                for k in range(PACK):
+                    nc.tensor.transpose(back[:, k, :], wide[:, k].rearrange("j g r -> j (g r)"), ident[:])
+                nc.scalar.copy(wgt_sb[:, CH * c : CH * (c + 1)], back[:].rearrange("p k j -> p (k j)"))
 
         def load_plane(a, i):
             planes[a, i] = tagged("plane", [P, T], F32)
@@ -78,17 +101,23 @@ def tile_list_relation_type_max_kernel(
 
         wb, wq, xb, xq, g, tg_w = {}, {}, {}, {}, {}, {}
 
-        def cast_wx(a, b, copy):
-            wb[a, b] = tagged("b16", [P, KP * PACK], BF16)
+        def cast_wx(a, b, copy, t0=0, t1=PACK):
+            if (a, b) not in wb:
+                wb[a, b] = tagged("b16", [P, KP * PACK], BF16)
             copy(
-                wb[a, b][:].rearrange("p (t m j) -> p m j t", t=PACK, j=PACK),
-                wx_raw[a, b][:].rearrange("p j (m t) -> p m j t", t=PACK),
+                wb[a, b][:].rearrange("p (t m j) -> p m j t", t=PACK, j=PACK)[:, :, :, t0:t1],
+                wx_raw[a, b][:].rearrange("p j (m t) -> p m j t", t=PACK)[:, :, :, t0:t1],
             )
 
-        def quantize(name, src, tag):
-            codes = tagged(tag, [P, CH], U32)
-            scales = kept(name + "_s", [P, CH], U8)
-            nc.vector.quantize_mx(out=codes[:].bitcast(FP8X4), scales=scales[:], in_=src[:])
+        made = {}
+
+        def quantize(name, src, tag, lo=0, hi=CH):
+            if name not in made:
+                made[name] = tagged(tag, [P, CH], U32), kept(name + "_s", [P, CH], U8)
+            codes, scales = made[name]
+            nc.vector.quantize_mx(
+                out=codes[:, lo:hi].bitcast(FP8X4), scales=scales[:, lo:hi], in_=src[:]
+            )
             return codes, scales
 
         def new_quad(a, c):
@@ -111,11 +140,11 @@ def tile_list_relation_type_max_kernel(
                 ALU.mult,
             )
 
-        def interleave(a, c):
-            xb[a, c] = tagged("b16", [P, CH * PACK], BF16)
+        def interleave(a, c, lo=0, hi=CH):
+            xb[a, c, lo] = xb[a, c] = tagged("b16", [P, (hi - lo) * PACK], BF16)
             nc.scalar.copy(
-                xb[a, c][:].rearrange("p (c i t) -> p c t i", i=4, t=PACK),
-                g[a, c][:].rearrange("p t (c i) -> p c t i", i=4),
+                xb[a, c, lo][:].rearrange("p (c i t) -> p c t i", i=4, t=PACK),
+                g[a, c][:, :, lo:hi].rearrange("p t (c i) -> p c t i", i=4),
             )
 
         def interleave_pair(a, c, u, lo, hi):
@@ -124,7 +153,12 @@ def tile_list_relation_type_max_kernel(
             dst = xb[a, c][:, PACK * lo : PACK * hi].rearrange("p (n t) -> p n t", t=PACK)[:, :, 2 * u : 2 * u + 2]
             nc.scalar.copy(dst, g[a, c, "pair", u][:, :, lo:hi].rearrange("p t n -> p n t"))
 
-        tg_s = kept("tg_s", [P, S], U8)
+        tg_s = {}
+
+        def gather_tab_scales(c, tag):
+            tg_s[c] = tagged(tag, [P, CH], U8)
+            cols = slice(CH * c // 16, CH * (c + 1) // 16)
+            nc.vector.tensor_copy(tg_s[c][:], tab_sc[:].bitcast(U8).indirect(offs_sb[:, cols]))
 
         def gather_tab_words(c, tag):
             tg_w[c] = tagged(tag, [P, CH], U32)
@@ -132,7 +166,7 @@ def tile_list_relation_type_max_kernel(
             nc.vector.tensor_copy(tg_w[c][:], tab_w[:].bitcast(U32).indirect(offs_sb[:, cols]))
 
         wt_p = kept("wt_p", [P, 2 * H], U8)
-        wt_sc = kept("wt_sc", [P, H], U8)
+        wt_sc = tagged("codes", [P, H], U8)
 
         def permute_wt_words():
             nc.vector.tensor_copy(
@@ -165,7 +199,35 @@ def tile_list_relation_type_max_kernel(
                     )
                 nc.scalar.activation(biased[c, b][:, t, lo:hi], acc[:], ACT.Identity, bias=bx_sb[:, b, t : t + 1])
 
-        def join(c, b, q):
+        p_sb = {}
+
+        def project_types(c, b):
+            p_sb[c, b] = tagged("p_sb", [P, PACK, CH], F32)
+            for t in range(PACK):
+                col = KP * b + P * t
+                acc = psum.tile([P, CH], F32, name="acc", bufs=bufs["acc"])
+                nc.tensor.matmul_mx(
+                    out=acc[:],
+                    lhsT=wt_p[:, 2 * col : 2 * (col + P)].bitcast(FP4X4),
+                    lhsT_scale=wt_sc[:, col : col + P],
+                    rhs=tg_w[c][:].bitcast(FP8X4),
+                    rhs_scale=tg_s[c][:],
+                    start=True,
+                    stop=True,
+                )
+                nc.scalar.copy(p_sb[c, b][:, t, :], acc[:])
+
+        def join(c, b, lo=0, hi=CH):
+            if (c, b) not in hb:
+                hb[c, b] = tagged("b16", [P, CH * PACK], BF16)
+            nc.vector.tensor_tensor(
+                hb[c, b][:, PACK * lo : PACK * hi].rearrange("p (c i t) -> p c t i", i=4, t=PACK),
+                p_sb[c, b][:, :, lo:hi].rearrange("p t (c i) -> p c t i", i=4),
+                biased[c, b][:, :, lo:hi].rearrange("p t (c i) -> p c t i", i=4),
+                ALU.max,
+            )
+
+        def join_from_psum(c, b, q):
             if (c, b) not in hb:
                 hb[c, b] = tagged("b16", [P, CH * PACK], BF16)
             pb = psum.tile([P, PACK, P], F32, name="pb", bufs=bufs["pb"])
@@ -176,7 +238,7 @@ def tile_list_relation_type_max_kernel(
                     lhsT=wt_p[:, 2 * col : 2 * (col + P)].bitcast(FP4X4),
                     lhsT_scale=wt_sc[:, col : col + P],
                     rhs=tg_w[c][:, P * q : P * (q + 1)].bitcast(FP8X4),
-                    rhs_scale=tg_s[:, CH * c + P * q : CH * c + P * (q + 1)],
+                    rhs_scale=tg_s[c][:, P * q : P * (q + 1)],
                     start=True,
                     stop=True,
                 )
@@ -221,11 +283,12 @@ def tile_list_relation_type_max_kernel(
 
         nc.sync.dma_start(wt_raw[:], wt_words[0].bitcast(I32))
         nc.sync.dma_start(offs_sb[:], offs)
+        load_edge_weights()
         load_scale_rows(tab_sc, tab_scales[0])
+        nc.sync.dma_start(tab_w[:], tab_words[0].rearrange("p t i -> p (t i)").bitcast(I32))
+        load_scale_rows(wt_sc_raw, wt_scales[0])
         nc.sync.dma_start(offs2_sb[:], offs2)
         load_plane(0, 0)
-        load_scale_rows(wt_sc_raw, wt_scales[0])
-        nc.sync.dma_start(wgt_sb[:], wgt)
         load_plane(0, 1)
         load_plane(0, 2)
         load_plane(0, 3)
@@ -236,16 +299,22 @@ def tile_list_relation_type_max_kernel(
         load_plane(1, 2)
         load_wx(0, 1)
         load_plane(1, 3)
-        nc.sync.dma_start(bx_sb[:], bx.rearrange("(b p t) -> p b t", b=2, t=PACK))
-        nc.sync.dma_start(tab_w[:], tab_words[0].rearrange("p t i -> p (t i)").bitcast(I32))
         load_wx(1, 1)
+        nc.sync.dma_start(bx_sb[:], bx.rearrange("(b p t) -> p b t", b=2, t=PACK))
         load_scale_rows(wo_sc, wo_scales.rearrange("a r n -> r a n"))
         nc.sync.dma_start(wo_w[:], wo_words.rearrange("a p n t -> p a (n t)").bitcast(I32))
         with nc.allow_non_contiguous_dma(reason="one bias value to a partition"):
             nc.sync.dma_start(bo_sb[:], bo.rearrange("(c p) -> p c", p=P))
-        nc.vector.tensor_copy(tg_s[:], tab_sc[:].bitcast(U8).indirect(offs_sb[:]))
-        permute_wt_scales()
+        spread_edge_weights()
         permute_wt_words()
+        gather_tab_scales(0, "tgs")
+        gather_tab_scales(1, "tgs")
+        permute_wt_scales()
+        gather_tab_words(0, "codes")
+        gather_tab_words(1, "codes")
+        for c in range(NCH):
+            for b in range(2):
+                project_types(c, b)
         new_quad(0, 0)
         new_quad(0, 1)
         for i in range(PACK):
@@ -265,8 +334,8 @@ def tile_list_relation_type_max_kernel(
         gather(1, 1, 0)
         gather(1, 1, 1)
         xq[0, 1] = quantize("xq01", xb[0, 1], "codes")
-        interleave_pair(1, 0, 0, 0, CH)
         cast_wx(1, 0, nc.scalar.copy)
+        interleave_pair(1, 0, 0, 0, CH)
         new_pair(1, 0, 1)
         gather(1, 2, 0)
         gather(1, 2, 1)
@@ -277,26 +346,35 @@ def tile_list_relation_type_max_kernel(
         gather(1, 3, 0, 256, 512)
         interleave_pair(1, 0, 1, 256, 512)
         gather(1, 3, 1)
-        xq[1, 0] = quantize("xq10", xb[1, 0], "codes")
-        wq[0, 1] = quantize("wq01", wb[0, 1], "codes")
         interleave(1, 1)
-        gather_tab_words(0, "codes")
-        xq[1, 1] = quantize("xq11", xb[1, 1], "codes")
+        wq[0, 1] = quantize("wq01", wb[0, 1], "b16")
+        xq[1, 0] = quantize("xq10", xb[1, 0], "codes")
         cast_wx(1, 1, nc.vector.tensor_copy)
-        gather_tab_words(1, "b16")
+        xq[1, 1] = quantize("xq11", xb[1, 1], "b16")
         wq[1, 1] = quantize("wq11", wb[1, 1], "codes")
-        for c, b in ((0, 0), (1, 0), (0, 1)):
-            project_x(c, b)
-            for q in range(4):
-                join(c, b, q)
-        project_x(1, 1)
+        for b in range(2):
+            for lo in (0, 256):
+                project_x(0, b, lo, lo + 256)
+        join(0, 0, 0, 256)
+        join(0, 0, 256, CH)
+        join(0, 1, 0, 256)
         quantize_h(0, 0, "codes")
+        join(0, 1, 256, CH)
+        project_x(1, 0, 0, 256)
+        project_x(1, 0, 256, CH)
+        join(1, 0, 0, 256)
         quantize_h(0, 1, "codes")
-        for q in range(4):
-            join(1, 1, q)
+        join(1, 0, 256, CH)
+        project_x(1, 1)
+        for nt in range(4):
+            project_h(0, 0, CH, [nt])
+        join(1, 1, 0, 256)
         quantize_h(1, 0, "codes")
+        join(1, 1, 256, CH)
+        update(0, 0, CH, [0], nc.vector)
         quantize_h(1, 1, "codes")
-        for c in range(NCH):
-            for nt in range(4):
-                project_h(c, 0, CH, [nt])
-                update(c, 0, CH, [nt], nc.vector)
+        for nt in range(1, 4):
+            update(0, 0, CH, [nt], nc.vector)
+        for nt in range(4):
+            project_h(1, 0, CH, [nt])
+            update(1, 0, CH, [nt], nc.vector)

@@ -35,7 +35,7 @@ def tile_list_relation_type_max_kernel(
         keep = ctx.enter_context(tc.tile_pool(name="keep", bufs=1))
         ring = ctx.enter_context(tc.tile_pool(name="ring", bufs=2))
         psum = ctx.enter_context(tc.psum_pool(name="psum", bufs=1))
-        bufs = {"plane": 5, "wx_raw": 3, "b16": 8, "tgs": 2, "codes": 12, "pair": 4, "f32x4": 4, "p_sb": 4, "th": 5, "acc": 8}
+        bufs = {"plane": 5, "wx_raw": 3, "b16": 9, "tgs": 2, "codes": 12, "pair": 4, "f32x4": 4, "p_sb": 4, "th": 5, "acc": 8}
 
         def kept(name, shape, dtype):
             return keep.tile(shape, dtype, name=name, align_bytes=64)
@@ -346,12 +346,13 @@ def tile_list_relation_type_max_kernel(
         gather(1, 3, 0, 256, 512)
         interleave_pair(1, 0, 1, 256, 512)
         gather(1, 3, 1)
-        interleave(1, 1)
-        wq[0, 1] = quantize("wq01", wb[0, 1], "b16")
-        xq[1, 0] = quantize("xq10", xb[1, 0], "codes")
+        interleave(1, 1, 0, 256)
+        xq[1, 0] = quantize("xq10", xb[1, 0][:, 0:1024], "b16", 0, 256)
+        quantize("xq10", xb[1, 0][:, 1024:2048], "b16", 256, CH)
         cast_wx(1, 1, nc.vector.tensor_copy)
-        xq[1, 1] = quantize("xq11", xb[1, 1], "b16")
+        wq[0, 1] = quantize("wq01", wb[0, 1], "b16")
         wq[1, 1] = quantize("wq11", wb[1, 1], "codes")
+        xq[1, 1] = quantize("xq11", xb[1, 1, 0], "codes", 0, 256)
         for b in range(2):
             for lo in (0, 256):
                 project_x(0, b, lo, lo + 256)
@@ -360,17 +361,20 @@ def tile_list_relation_type_max_kernel(
         join(0, 1, 0, 256)
         quantize_h(0, 0, "codes")
         join(0, 1, 256, CH)
+        interleave(1, 1, 256, CH)
         project_x(1, 0, 0, 256)
-        project_x(1, 0, 256, CH)
+        project_x(1, 1, 0, 256)
+        quantize("xq11", xb[1, 1, 256], "codes", 256, CH)
         join(1, 0, 0, 256)
         quantize_h(0, 1, "codes")
-        join(1, 0, 256, CH)
-        project_x(1, 1)
+        project_x(1, 0, 256, CH)
+        project_x(1, 1, 256, CH)
         for nt in range(4):
             project_h(0, 0, CH, [nt])
         join(1, 1, 0, 256)
-        quantize_h(1, 0, "codes")
+        join(1, 0, 256, CH)
         join(1, 1, 256, CH)
+        quantize_h(1, 0, "codes")
         update(0, 0, CH, [0], nc.vector)
         quantize_h(1, 1, "codes")
         for nt in range(1, 4):

@@ -35,7 +35,7 @@ def tile_list_relation_type_max_kernel(
         keep = ctx.enter_context(tc.tile_pool(name="keep", bufs=1))
         ring = ctx.enter_context(tc.tile_pool(name="ring", bufs=2))
         psum = ctx.enter_context(tc.psum_pool(name="psum", bufs=1))
-        bufs = {"plane": 5, "wx_raw": 3, "b16": 9, "tgs": 2, "codes": 12, "pair": 4, "f32x4": 4, "p_sb": 4, "th": 5, "acc": 8}
+        bufs = {"plane": 5, "wx_raw": 3, "b16": 9, "tgs": 2, "codes": 11, "pair": 4, "f32x4": 4, "p_sb": 4, "th": 5, "acc": 8}
 
         def kept(name, shape, dtype):
             return keep.tile(shape, dtype, name=name, align_bytes=64)
@@ -166,16 +166,16 @@ def tile_list_relation_type_max_kernel(
             nc.vector.tensor_copy(tg_w[c][:], tab_w[:].bitcast(U32).indirect(offs_sb[:, cols]))
 
         wt_p = kept("wt_p", [P, 2 * H], U8)
-        wt_sc = tagged("codes", [P, H], U8)
+        wt_sc = kept("wt_sc", [P, H], U8)
 
         def permute_wt_words():
-            nc.vector.tensor_copy(
+            nc.gpsimd.tensor_copy(
                 wt_p[:].bitcast(U16).rearrange("p (b t m) -> p b m t", b=2, t=PACK),
                 wt_raw[:].bitcast(U16).rearrange("p (b m t) -> p b m t", b=2, t=PACK),
             )
 
         def permute_wt_scales():
-            nc.vector.tensor_copy(
+            nc.gpsimd.tensor_copy(
                 wt_sc[:].rearrange("p (b t m) -> p b m t", b=2, t=PACK),
                 wt_sc_raw[:].bitcast(U8).rearrange("p (b m t) -> p b m t", b=2, t=PACK),
             )
@@ -281,10 +281,10 @@ def tile_list_relation_type_max_kernel(
             dst = out[P * nts[0] : P * (nts[-1] + 1), CH * c + lo : CH * c + hi].rearrange("(c p) j -> p c j", p=P)
             nc.sync.dma_start(dst, rows)
 
-        nc.sync.dma_start(wt_raw[:], wt_words[0].bitcast(I32))
         nc.sync.dma_start(offs_sb[:], offs)
-        load_edge_weights()
         load_scale_rows(tab_sc, tab_scales[0])
+        nc.sync.dma_start(wt_raw[:], wt_words[0].bitcast(I32))
+        load_edge_weights()
         nc.sync.dma_start(tab_w[:], tab_words[0].rearrange("p t i -> p (t i)").bitcast(I32))
         load_scale_rows(wt_sc_raw, wt_scales[0])
         nc.sync.dma_start(offs2_sb[:], offs2)

@@ -170,14 +170,14 @@ def tile_list_relation_type_max_kernel(
 
         def permute_wt_words():
             nc.gpsimd.tensor_copy(
-                wt_p[:].bitcast(U16).rearrange("p (b t m) -> p b m t", b=2, t=PACK),
-                wt_raw[:].bitcast(U16).rearrange("p (b m t) -> p b m t", b=2, t=PACK),
+                wt_p[:].bitcast(U16).rearrange("p (b t m) -> p b t m", b=2, t=PACK),
+                wt_raw[:].bitcast(U16).rearrange("p (b m t) -> p b t m", b=2, t=PACK),
             )
 
         def permute_wt_scales():
             nc.gpsimd.tensor_copy(
-                wt_sc[:].rearrange("p (b t m) -> p b m t", b=2, t=PACK),
-                wt_sc_raw[:].bitcast(U8).rearrange("p (b m t) -> p b m t", b=2, t=PACK),
+                wt_sc[:].rearrange("p (b t m) -> p b t m", b=2, t=PACK),
+                wt_sc_raw[:].bitcast(U8).rearrange("p (b m t) -> p b t m", b=2, t=PACK),
             )
 
         hq, biased, hb = {}, {}, {}

@@ -90,10 +90,10 @@ def tile_list_relation_type_max_kernel(
             rows = xT[KP * a : KP * (a + 1), :].rearrange("(p i) t -> p i t", i=PACK)
             nc.sync.dma_start(planes[a, i][:], rows[:, i, :])
 
-        def load_wx(a, b):
-            wx_raw[a, b] = tagged("wx_raw", [P, PACK, KP], F32)
-            rows = wx[KP * a : KP * (a + 1), KP * b : KP * (b + 1)].rearrange("(p j) c -> p j c", j=PACK)
-            nc.sync.dma_start(wx_raw[a, b][:], rows)
+        def load_wx(a, b, lo=0, hi=KP):
+            wx_raw[a, b, lo] = tagged("wx_raw", [P, PACK, hi - lo], F32)
+            rows = wx[KP * a : KP * (a + 1), KP * b + lo : KP * b + hi].rearrange("(p j) c -> p j c", j=PACK)
+            nc.sync.dma_start(wx_raw[a, b, lo][:], rows)
 
         def load_old(c):
             old_sb[c] = tagged("plane", [P, N // P, CH], F32)
@@ -101,12 +101,12 @@ def tile_list_relation_type_max_kernel(
 
         wb, wq, xb, xq, g, tg_w = {}, {}, {}, {}, {}, {}
 
-        def cast_wx(a, b, copy, t0=0, t1=PACK):
+        def cast_wx(a, b, copy, lo=0, hi=KP):
             if (a, b) not in wb:
                 wb[a, b] = tagged("b16", [P, KP * PACK], BF16)
             copy(
-                wb[a, b][:].rearrange("p (t m j) -> p m j t", t=PACK, j=PACK)[:, :, :, t0:t1],
-                wx_raw[a, b][:].rearrange("p j (m t) -> p m j t", t=PACK)[:, :, :, t0:t1],
+                wb[a, b][:].rearrange("p (t m j) -> p m j t", t=PACK, j=PACK)[:, lo // PACK : hi // PACK],
+                wx_raw[a, b, lo][:].rearrange("p j (m t) -> p m j t", t=PACK),
             )
 
         made = {}
@@ -125,6 +125,15 @@ def tile_list_relation_type_max_kernel(
             g[a, c] = quad
             for i in range(PACK):
                 g[a, c, i] = quad[:, i, :]
+
+        def new_wide_quad(a):
+            quad = tagged("wide", [P, PACK, S], F32)
+            g[a] = quad
+            for c in range(NCH):
+                g[a, c] = quad[:, :, CH * c : CH * (c + 1)]
+
+        def gather_all(a, i):
+            nc.vector.tensor_tensor(g[a][:, i, :], planes[a, i][:].indirect(offs2_sb[:]), wgt_sb[:], ALU.mult)
 
         def new_pair(a, c, u):
             pair = tagged("pair", [P, 2, CH], F32)
@@ -297,8 +306,9 @@ def tile_list_relation_type_max_kernel(
         load_plane(1, 1)
         load_wx(1, 0)
         load_plane(1, 2)
-        load_wx(0, 1)
+        load_wx(0, 1, 0, 256)
         load_plane(1, 3)
+        load_wx(0, 1, 256, 512)
         load_wx(1, 1)
         nc.sync.dma_start(bx_sb[:], bx.rearrange("(b p t) -> p b t", b=2, t=PACK))
         load_scale_rows(wo_sc, wo_scales.rearrange("a r n -> r a n"))
@@ -340,7 +350,7 @@ def tile_list_relation_type_max_kernel(
         gather(1, 2, 0)
         gather(1, 2, 1)
         wq[1, 0] = quantize("wq10", wb[1, 0], "pair")
-        cast_wx(0, 1, nc.scalar.copy)
+        cast_wx(0, 1, nc.scalar.copy, 0, 256)
         gather(1, 3, 0, 0, 256)
         interleave_pair(1, 0, 1, 0, 256)
         gather(1, 3, 0, 256, 512)
@@ -349,36 +359,46 @@ def tile_list_relation_type_max_kernel(
         interleave(1, 1, 0, 256)
         xq[1, 0] = quantize("xq10", xb[1, 0][:, 0:1024], "b16", 0, 256)
         quantize("xq10", xb[1, 0][:, 1024:2048], "b16", 256, CH)
+        cast_wx(0, 1, nc.vector.tensor_copy, 256, 512)
         cast_wx(1, 1, nc.vector.tensor_copy)
         wq[0, 1] = quantize("wq01", wb[0, 1], "b16")
         wq[1, 1] = quantize("wq11", wb[1, 1], "codes")
         xq[1, 1] = quantize("xq11", xb[1, 1, 0], "codes", 0, 256)
-        for b in range(2):
-            for lo in (0, 256):
-                project_x(0, b, lo, lo + 256)
+        project_x(0, 0, 0, 256)
+        project_x(0, 0, 256, 512)
+        project_x(0, 1, 0, 256)
+        project_x(0, 1, 256, 512)
         join(0, 0, 0, 256)
-        join(0, 0, 256, CH)
+        join(0, 0, 256, 512)
         join(0, 1, 0, 256)
         quantize_h(0, 0, "codes")
-        join(0, 1, 256, CH)
+        join(0, 1, 256, 512)
         interleave(1, 1, 256, CH)
         project_x(1, 0, 0, 256)
         project_x(1, 1, 0, 256)
         quantize("xq11", xb[1, 1, 256], "codes", 256, CH)
         join(1, 0, 0, 256)
         quantize_h(0, 1, "codes")
-        project_x(1, 0, 256, CH)
-        project_x(1, 1, 256, CH)
-        for nt in range(4):
-            project_h(0, 0, CH, [nt])
+        project_x(1, 0, 256, 512)
+        project_x(1, 1, 256, 512)
+        project_h(0, 0, CH, [0])
+        project_h(0, 0, CH, [1])
+        project_h(0, 0, CH, [2])
+        project_h(0, 0, CH, [3])
         join(1, 1, 0, 256)
-        join(1, 0, 256, CH)
-        join(1, 1, 256, CH)
+        join(1, 0, 256, 512)
         quantize_h(1, 0, "codes")
+        join(1, 1, 256, 512)
         update(0, 0, CH, [0], nc.vector)
         quantize_h(1, 1, "codes")
-        for nt in range(1, 4):
-            update(0, 0, CH, [nt], nc.vector)
-        for nt in range(4):
-            project_h(1, 0, CH, [nt])
-            update(1, 0, CH, [nt], nc.vector)
+        update(0, 0, CH, [1], nc.vector)
+        update(0, 0, CH, [2], nc.vector)
+        update(0, 0, CH, [3], nc.vector)
+        project_h(1, 0, CH, [0])
+        update(1, 0, CH, [0], nc.vector)
+        project_h(1, 0, CH, [1])
+        update(1, 0, CH, [1], nc.vector)
+        project_h(1, 0, CH, [2])
+        update(1, 0, CH, [2], nc.vector)
+        project_h(1, 0, CH, [3])
+        update(1, 0, CH, [3], nc.vector)

@@ -24,6 +24,7 @@ CH = 512
 NCH = S // CH
 R, GROUP = 8, 16
 NB = S // P
+QT = 256
 
 
 def tile_list_relation_type_max_kernel(
@@ -35,7 +36,7 @@ def tile_list_relation_type_max_kernel(
         keep = ctx.enter_context(tc.tile_pool(name="keep", bufs=1))
         ring = ctx.enter_context(tc.tile_pool(name="ring", bufs=2))
         psum = ctx.enter_context(tc.psum_pool(name="psum", bufs=1))
-        bufs = {"plane": 5, "wx_raw": 3, "b16": 9, "tgs": 2, "codes": 11, "pair": 4, "f32x4": 4, "p_sb": 4, "th": 5, "acc": 8}
+        bufs = {"plane": 4, "held": 1, "wx_raw": 3, "b16": 9, "tgs": 2, "codes": 11, "pair": 4, "f32x4": 4, "p_sb": 4, "th": 5, "acc": 8}
 
         def kept(name, shape, dtype):
             return keep.tile(shape, dtype, name=name, align_bytes=64)
@@ -85,8 +86,8 @@ def tile_list_relation_type_max_kernel(
                     nc.tensor.transpose(back[:, k, :], wide[:, k].rearrange("j g r -> j (g r)"), ident[:])
                 nc.scalar.copy(wgt_sb[:, CH * c : CH * (c + 1)], back[:].rearrange("p k j -> p (k j)"))
 
-        def load_plane(a, i):
-            planes[a, i] = tagged("plane", [P, T], F32)
+        def load_plane(a, i, tag="plane"):
+            planes[a, i] = tagged(tag, [P, T], F32)
             rows = xT[KP * a : KP * (a + 1), :].rearrange("(p i) t -> p i t", i=PACK)
             nc.sync.dma_start(planes[a, i][:], rows[:, i, :])
 
@@ -113,7 +114,7 @@ def tile_list_relation_type_max_kernel(
 
         def quantize(name, src, tag, lo=0, hi=CH):
             if name not in made:
-                made[name] = tagged(tag, [P, CH], U32), kept(name + "_s", [P, CH], U8)
+                made[name] = tagged(tag, [P, CH], U32)[:], kept(name + "_s", [P, CH], U8)
             codes, scales = made[name]
             nc.vector.quantize_mx(
                 out=codes[:, lo:hi].bitcast(FP8X4), scales=scales[:, lo:hi], in_=src[:]
@@ -125,15 +126,6 @@ def tile_list_relation_type_max_kernel(
             g[a, c] = quad
             for i in range(PACK):
                 g[a, c, i] = quad[:, i, :]
-
-        def new_wide_quad(a):
-            quad = tagged("wide", [P, PACK, S], F32)
-            g[a] = quad
-            for c in range(NCH):
-                g[a, c] = quad[:, :, CH * c : CH * (c + 1)]
-
-        def gather_all(a, i):
-            nc.vector.tensor_tensor(g[a][:, i, :], planes[a, i][:].indirect(offs2_sb[:]), wgt_sb[:], ALU.mult)
 
         def new_pair(a, c, u):
             pair = tagged("pair", [P, 2, CH], F32)
@@ -183,10 +175,10 @@ def tile_list_relation_type_max_kernel(
                 wt_raw[:].bitcast(U16).rearrange("p (b m t) -> p b t m", b=2, t=PACK),
             )
 
-        def permute_wt_scales():
+        def permute_wt_scales(b):
             nc.gpsimd.tensor_copy(
-                wt_sc[:].rearrange("p (b t m) -> p b t m", b=2, t=PACK),
-                wt_sc_raw[:].bitcast(U8).rearrange("p (b m t) -> p b t m", b=2, t=PACK),
+                wt_sc[:, KP * b : KP * (b + 1)].rearrange("p (t m) -> p t m", t=PACK),
+                wt_sc_raw[:].bitcast(U8)[:, KP * b : KP * (b + 1)].rearrange("p (m t) -> p t m", t=PACK),
             )
 
         hq, biased, hb = {}, {}, {}
@@ -236,27 +228,22 @@ def tile_list_relation_type_max_kernel(
                 ALU.max,
             )
 
-        def join_from_psum(c, b, q):
-            if (c, b) not in hb:
-                hb[c, b] = tagged("b16", [P, CH * PACK], BF16)
-            pb = psum.tile([P, PACK, P], F32, name="pb", bufs=bufs["pb"])
-            for t in range(PACK):
-                col = KP * b + P * t
-                nc.tensor.matmul_mx(
-                    out=pb[:, t, :],
-                    lhsT=wt_p[:, 2 * col : 2 * (col + P)].bitcast(FP4X4),
-                    lhsT_scale=wt_sc[:, col : col + P],
-                    rhs=tg_w[c][:, P * q : P * (q + 1)].bitcast(FP8X4),
-                    rhs_scale=tg_s[c][:, P * q : P * (q + 1)],
-                    start=True,
-                    stop=True,
-                )
+        def join_quarter(q, b):
+            c, lo = divmod(QT * q, CH)
+            if q not in hb:
+                hb[q] = tagged("b16", [P, 2, QT * PACK], BF16)
             nc.vector.tensor_tensor(
-                hb[c, b][:, PACK * P * q : PACK * P * (q + 1)].rearrange("p (c i t) -> p c t i", i=4, t=PACK),
-                pb[:].rearrange("p t (c i) -> p c t i", i=4),
-                biased[c, b][:, :, P * q : P * (q + 1)].rearrange("p t (c i) -> p c t i", i=4),
+                hb[q][:, b, :].rearrange("p (c i t) -> p c t i", i=4, t=PACK),
+                p_sb[c, b][:, :, lo : lo + QT].rearrange("p t (c i) -> p c t i", i=4),
+                biased[c, b][:, :, lo : lo + QT].rearrange("p t (c i) -> p c t i", i=4),
                 ALU.max,
             )
+
+        def quantize_quarter(q):
+            codes, scales = tagged("codes", [P, 2 * QT], U32), kept("hq_q%d_s" % q, [P, 2 * QT], U8)
+            nc.vector.quantize_mx(out=codes[:].bitcast(FP8X4), scales=scales[:], in_=hb[q][:].rearrange("p b n -> p (b n)"))
+            for b in range(2):
+                hq["q", q, b] = codes[:, QT * b : QT * (b + 1)], scales[:, QT * b : QT * (b + 1)]
 
         def quantize_h(c, b, tag, lo=0, hi=CH):
             if (c, b) not in hq:
@@ -270,6 +257,10 @@ def tile_list_relation_type_max_kernel(
 
         def project_h(c, lo, hi, nts):
             th[c, lo, nts[0]] = tagged("th", [P, len(nts), hi - lo], F32)
+            if c == 0:
+                h_ops = [(hq[c, b][0][:, lo:hi], hq[c, b][1][:, lo:hi]) for b in range(2)]
+            else:
+                h_ops = [hq["q", (CH * c + lo) // QT, b] for b in range(2)]
             for k, nt in enumerate(nts):
                 acc = psum.tile([P, hi - lo], F32, name="acc", bufs=bufs["acc"])
                 for b in range(2):
@@ -277,23 +268,25 @@ def tile_list_relation_type_max_kernel(
                         out=acc[:],
                         lhsT=wo_w[:, b, P * nt : P * (nt + 1)].bitcast(FP8X4),
                         lhsT_scale=wo_sc[:, b, :].bitcast(U8)[:, P * nt : P * (nt + 1)],
-                        rhs=hq[c, b][0][:, lo:hi].bitcast(FP8X4),
-                        rhs_scale=hq[c, b][1][:, lo:hi],
+                        rhs=h_ops[b][0].bitcast(FP8X4),
+                        rhs_scale=h_ops[b][1],
                         start=(b == 0),
                         stop=(b == 1),
                     )
                 nc.scalar.activation(th[c, lo, nts[0]][:, k, :], acc[:], ACT.Tanh, bias=bo_sb[:, nt : nt + 1])
 
-        def update(c, lo, hi, nts, adder):
+        def update(c, lo, hi, nts, adder, parts=1):
             rows = old_sb[c][:, nts[0] : nts[-1] + 1, lo:hi]
-            adder.tensor_tensor(rows, rows, th[c, lo, nts[0]][:], ALU.add)
+            step = (hi - lo) // parts
+            for k in range(0, hi - lo, step):
+                adder.tensor_tensor(rows[:, :, k : k + step], rows[:, :, k : k + step], th[c, lo, nts[0]][:, :, k : k + step], ALU.add)
             dst = out[P * nts[0] : P * (nts[-1] + 1), CH * c + lo : CH * c + hi].rearrange("(c p) j -> p c j", p=P)
             nc.sync.dma_start(dst, rows)
 
         nc.sync.dma_start(offs_sb[:], offs)
-        load_scale_rows(tab_sc, tab_scales[0])
         nc.sync.dma_start(wt_raw[:], wt_words[0].bitcast(I32))
         load_edge_weights()
+        load_scale_rows(tab_sc, tab_scales[0])
         nc.sync.dma_start(tab_w[:], tab_words[0].rearrange("p t i -> p (t i)").bitcast(I32))
         load_scale_rows(wt_sc_raw, wt_scales[0])
         nc.sync.dma_start(offs2_sb[:], offs2)
@@ -303,7 +296,7 @@ def tile_list_relation_type_max_kernel(
         load_plane(0, 3)
         load_wx(0, 0)
         load_plane(1, 0)
-        load_plane(1, 1)
+        load_plane(1, 1, "held")
         load_wx(1, 0)
         load_plane(1, 2)
         load_wx(0, 1, 0, 256)
@@ -319,11 +312,12 @@ def tile_list_relation_type_max_kernel(
         permute_wt_words()
         gather_tab_scales(0, "tgs")
         gather_tab_scales(1, "tgs")
-        permute_wt_scales()
+        permute_wt_scales(0)
+        permute_wt_scales(1)
         gather_tab_words(0, "codes")
         gather_tab_words(1, "codes")
-        for c in range(NCH):
-            for b in range(2):
+        for b in range(2):
+            for c in range(NCH):
                 project_types(c, b)
         new_quad(0, 0)
         new_quad(0, 1)
@@ -339,11 +333,14 @@ def tile_list_relation_type_max_kernel(
         new_quad(1, 1)
         gather(1, 0, 0)
         gather(1, 0, 1)
-        wq[0, 0] = quantize("wq00", wb[0, 0], "pair")
-        xq[0, 0] = quantize("xq00", xb[0, 0], "codes")
         gather(1, 1, 0)
         gather(1, 1, 1)
-        xq[0, 1] = quantize("xq01", xb[0, 1], "codes")
+        first_codes = tagged("held", [P, 3 * CH], U32)
+        for k, name in enumerate(["wq00", "xq00", "xq01"]):
+            made[name] = first_codes[:, CH * k : CH * (k + 1)], kept(name + "_s", [P, CH], U8)
+        wq[0, 0] = quantize("wq00", wb[0, 0], "held")
+        xq[0, 0] = quantize("xq00", xb[0, 0], "held")
+        xq[0, 1] = quantize("xq01", xb[0, 1], "held")
         cast_wx(1, 0, nc.scalar.copy)
         interleave_pair(1, 0, 0, 0, CH)
         new_pair(1, 0, 1)
@@ -356,14 +353,14 @@ def tile_list_relation_type_max_kernel(
         gather(1, 3, 0, 256, 512)
         interleave_pair(1, 0, 1, 256, 512)
         gather(1, 3, 1)
-        interleave(1, 1, 0, 256)
+        interleave(1, 1)
         xq[1, 0] = quantize("xq10", xb[1, 0][:, 0:1024], "b16", 0, 256)
         quantize("xq10", xb[1, 0][:, 1024:2048], "b16", 256, CH)
         cast_wx(0, 1, nc.vector.tensor_copy, 256, 512)
         cast_wx(1, 1, nc.vector.tensor_copy)
         wq[0, 1] = quantize("wq01", wb[0, 1], "b16")
         wq[1, 1] = quantize("wq11", wb[1, 1], "codes")
-        xq[1, 1] = quantize("xq11", xb[1, 1, 0], "codes", 0, 256)
+        xq[1, 1] = quantize("xq11", xb[1, 1], "codes")
         project_x(0, 0, 0, 256)
         project_x(0, 0, 256, 512)
         project_x(0, 1, 0, 256)
@@ -373,32 +370,32 @@ def tile_list_relation_type_max_kernel(
         join(0, 1, 0, 256)
         quantize_h(0, 0, "codes")
         join(0, 1, 256, 512)
-        interleave(1, 1, 256, CH)
         project_x(1, 0, 0, 256)
         project_x(1, 1, 0, 256)
-        quantize("xq11", xb[1, 1, 256], "codes", 256, CH)
-        join(1, 0, 0, 256)
+        join_quarter(2, 0)
         quantize_h(0, 1, "codes")
         project_x(1, 0, 256, 512)
         project_x(1, 1, 256, 512)
+        join_quarter(2, 1)
         project_h(0, 0, CH, [0])
         project_h(0, 0, CH, [1])
+        join_quarter(3, 0)
+        quantize_quarter(2)
         project_h(0, 0, CH, [2])
         project_h(0, 0, CH, [3])
-        join(1, 1, 0, 256)
-        join(1, 0, 256, 512)
-        quantize_h(1, 0, "codes")
-        join(1, 1, 256, 512)
+        join_quarter(3, 1)
         update(0, 0, CH, [0], nc.vector)
-        quantize_h(1, 1, "codes")
+        quantize_quarter(3)
+        project_h(1, 0, QT, [0, 1])
+        project_h(1, 0, QT, [2, 3])
         update(0, 0, CH, [1], nc.vector)
         update(0, 0, CH, [2], nc.vector)
         update(0, 0, CH, [3], nc.vector)
-        project_h(1, 0, CH, [0])
-        update(1, 0, CH, [0], nc.vector)
-        project_h(1, 0, CH, [1])
-        update(1, 0, CH, [1], nc.vector)
-        project_h(1, 0, CH, [2])
-        update(1, 0, CH, [2], nc.vector)
-        project_h(1, 0, CH, [3])
-        update(1, 0, CH, [3], nc.vector)
+        update(1, 0, QT, [0, 1], nc.vector)
+        update(1, 0, QT, [2, 3], nc.vector)
+        project_h(1, QT, CH, [0, 1])
+        update(1, QT, CH, [0, 1], nc.vector)
+        project_h(1, QT, CH, [2])
+        update(1, QT, CH, [2], nc.vector)
+        project_h(1, QT, CH, [3])
+        update(1, QT, CH, [3], nc.vector)

@@ -36,7 +36,7 @@ def tile_list_relation_type_max_kernel(
         keep = ctx.enter_context(tc.tile_pool(name="keep", bufs=1))
         ring = ctx.enter_context(tc.tile_pool(name="ring", bufs=2))
         psum = ctx.enter_context(tc.psum_pool(name="psum", bufs=1))
-        bufs = {"plane": 4, "held": 1, "wx_raw": 3, "b16": 9, "tgs": 2, "codes": 11, "pair": 4, "f32x4": 4, "p_sb": 4, "th": 5, "acc": 8}
+        bufs = {"plane": 5, "held": 1, "wx_raw": 3, "b16": 10, "tgs": 2, "codes": 10, "pair": 2, "f32x4": 4, "p_sb": 4, "th": 5, "acc": 8}
 
         def kept(name, shape, dtype):
             return keep.tile(shape, dtype, name=name, align_bytes=64)
@@ -96,6 +96,14 @@ def tile_list_relation_type_max_kernel(
             rows = wx[KP * a : KP * (a + 1), KP * b + lo : KP * b + hi].rearrange("(p j) c -> p j c", j=PACK)
             nc.sync.dma_start(wx_raw[a, b, lo][:], rows)
 
+        def load_wx_rows(a, u):
+            if a not in wx_raw:
+                wx_raw[a] = kept("wx_rows", [P, PACK, H], F32)
+                for b in range(2):
+                    wx_raw[a, b, 0] = wx_raw[a][:, :, KP * b : KP * (b + 1)]
+            rows = wx[KP * a : KP * (a + 1), :].rearrange("(p j) c -> p j c", j=PACK)
+            nc.sync.dma_start(wx_raw[a][:, 2 * u : 2 * u + 2, :], rows[:, 2 * u : 2 * u + 2, :])
+
         def load_old(c):
             old_sb[c] = tagged("plane", [P, N // P, CH], F32)
             nc.sync.dma_start(old_sb[c][:], old[:, CH * c : CH * (c + 1)].rearrange("(c p) j -> p c j", p=P))
@@ -141,10 +149,11 @@ def tile_list_relation_type_max_kernel(
                 ALU.mult,
             )
 
-        def interleave(a, c, lo=0, hi=CH):
-            xb[a, c, lo] = xb[a, c] = tagged("b16", [P, (hi - lo) * PACK], BF16)
-            nc.scalar.copy(
-                xb[a, c, lo][:].rearrange("p (c i t) -> p c t i", i=4, t=PACK),
+        def interleave(a, c, lo=0, hi=CH, copy=nc.scalar.copy):
+            if (a, c) not in xb:
+                xb[a, c] = tagged("b16", [P, CH * PACK], BF16)
+            copy(
+                xb[a, c][:, PACK * lo : PACK * hi].rearrange("p (c i t) -> p c t i", i=4, t=PACK),
                 g[a, c][:, :, lo:hi].rearrange("p t (c i) -> p c t i", i=4),
             )
 
@@ -294,16 +303,15 @@ def tile_list_relation_type_max_kernel(
         load_plane(0, 1)
         load_plane(0, 2)
         load_plane(0, 3)
-        load_wx(0, 0)
         load_plane(1, 0)
-        load_plane(1, 1, "held")
+        load_wx(0, 0)
+        load_plane(1, 1)
+        load_plane(1, 2, "held")
         load_wx(1, 0)
-        load_plane(1, 2)
-        load_wx(0, 1, 0, 256)
         load_plane(1, 3)
-        load_wx(0, 1, 256, 512)
-        load_wx(1, 1)
+        load_wx(0, 1)
         nc.sync.dma_start(bx_sb[:], bx.rearrange("(b p t) -> p b t", b=2, t=PACK))
+        load_wx(1, 1)
         load_scale_rows(wo_sc, wo_scales.rearrange("a r n -> r a n"))
         nc.sync.dma_start(wo_w[:], wo_words.rearrange("a p n t -> p a (n t)").bitcast(I32))
         with nc.allow_non_contiguous_dma(reason="one bias value to a partition"):
@@ -326,37 +334,34 @@ def tile_list_relation_type_max_kernel(
             gather(0, i, 1)
         load_old(0)
         load_old(1)
-        cast_wx(0, 0, nc.scalar.copy)
         interleave(0, 0)
         interleave(0, 1)
-        new_pair(1, 0, 0)
+        cast_wx(0, 0, nc.scalar.copy)
+        new_quad(1, 0)
         new_quad(1, 1)
         gather(1, 0, 0)
         gather(1, 0, 1)
+        xq[0, 0] = quantize("xq00", xb[0, 0], "codes")
         gather(1, 1, 0)
         gather(1, 1, 1)
-        first_codes = tagged("held", [P, 3 * CH], U32)
-        for k, name in enumerate(["wq00", "xq00", "xq01"]):
-            made[name] = first_codes[:, CH * k : CH * (k + 1)], kept(name + "_s", [P, CH], U8)
-        wq[0, 0] = quantize("wq00", wb[0, 0], "held")
-        xq[0, 0] = quantize("xq00", xb[0, 0], "held")
-        xq[0, 1] = quantize("xq01", xb[0, 1], "held")
         cast_wx(1, 0, nc.scalar.copy)
-        interleave_pair(1, 0, 0, 0, CH)
-        new_pair(1, 0, 1)
         gather(1, 2, 0)
         gather(1, 2, 1)
-        wq[1, 0] = quantize("wq10", wb[1, 0], "pair")
-        cast_wx(0, 1, nc.scalar.copy, 0, 256)
+        first_codes = tagged("held", [P, 2 * CH], U32)
+        for k, name in enumerate(["xq01", "wq00"]):
+            made[name] = first_codes[:, CH * k : CH * (k + 1)], kept(name + "_s", [P, CH], U8)
+        xq[0, 1] = quantize("xq01", xb[0, 1], "held")
+        wq[0, 0] = quantize("wq00", wb[0, 0], "held")
         gather(1, 3, 0, 0, 256)
-        interleave_pair(1, 0, 1, 0, 256)
+        interleave(1, 0, 0, 256)
         gather(1, 3, 0, 256, 512)
-        interleave_pair(1, 0, 1, 256, 512)
+        interleave(1, 0, 256, 512)
         gather(1, 3, 1)
         interleave(1, 1)
+        cast_wx(0, 1, nc.vector.tensor_copy)
+        wq[1, 0] = quantize("wq10", wb[1, 0], "b16")
         xq[1, 0] = quantize("xq10", xb[1, 0][:, 0:1024], "b16", 0, 256)
         quantize("xq10", xb[1, 0][:, 1024:2048], "b16", 256, CH)
-        cast_wx(0, 1, nc.vector.tensor_copy, 256, 512)
         cast_wx(1, 1, nc.vector.tensor_copy)
         wq[0, 1] = quantize("wq01", wb[0, 1], "b16")
         wq[1, 1] = quantize("wq11", wb[1, 1], "codes")

@@ -36,7 +36,7 @@ def tile_list_relation_type_max_kernel(
         keep = ctx.enter_context(tc.tile_pool(name="keep", bufs=1))
         ring = ctx.enter_context(tc.tile_pool(name="ring", bufs=2))
         psum = ctx.enter_context(tc.psum_pool(name="psum", bufs=1))
-        bufs = {"plane": 5, "held": 1, "wx_raw": 3, "b16": 10, "tgs": 2, "codes": 10, "pair": 2, "f32x4": 4, "p_sb": 4, "th": 5, "acc": 8}
+        bufs = {"plane": 5, "wx_raw": 4, "b16": 10, "tgs": 2, "codes": 10, "pair": 2, "f32x4": 4, "p_sb": 4, "th": 5, "acc": 8}
 
         def kept(name, shape, dtype):
             return keep.tile(shape, dtype, name=name, align_bytes=64)
@@ -115,7 +115,7 @@ def tile_list_relation_type_max_kernel(
                 wb[a, b] = tagged("b16", [P, KP * PACK], BF16)
             copy(
                 wb[a, b][:].rearrange("p (t m j) -> p m j t", t=PACK, j=PACK)[:, lo // PACK : hi // PACK],
-                wx_raw[a, b, lo][:].rearrange("p j (m t) -> p m j t", t=PACK),
+                wx_raw[a, b, 0][:, :, lo:hi].rearrange("p j (m t) -> p m j t", t=PACK),
             )
 
         made = {}
@@ -306,12 +306,12 @@ def tile_list_relation_type_max_kernel(
         load_plane(1, 0)
         load_wx(0, 0)
         load_plane(1, 1)
-        load_plane(1, 2, "held")
+        load_plane(1, 2)
         load_wx(1, 0)
         load_plane(1, 3)
         load_wx(0, 1)
-        nc.sync.dma_start(bx_sb[:], bx.rearrange("(b p t) -> p b t", b=2, t=PACK))
         load_wx(1, 1)
+        nc.sync.dma_start(bx_sb[:], bx.rearrange("(b p t) -> p b t", b=2, t=PACK))
         load_scale_rows(wo_sc, wo_scales.rearrange("a r n -> r a n"))
         nc.sync.dma_start(wo_w[:], wo_words.rearrange("a p n t -> p a (n t)").bitcast(I32))
         with nc.allow_non_contiguous_dma(reason="one bias value to a partition"):
@@ -344,14 +344,11 @@ def tile_list_relation_type_max_kernel(
         xq[0, 0] = quantize("xq00", xb[0, 0], "codes")
         gather(1, 1, 0)
         gather(1, 1, 1)
-        cast_wx(1, 0, nc.scalar.copy)
         gather(1, 2, 0)
         gather(1, 2, 1)
-        first_codes = tagged("held", [P, 2 * CH], U32)
-        for k, name in enumerate(["xq01", "wq00"]):
-            made[name] = first_codes[:, CH * k : CH * (k + 1)], kept(name + "_s", [P, CH], U8)
-        xq[0, 1] = quantize("xq01", xb[0, 1], "held")
-        wq[0, 0] = quantize("wq00", wb[0, 0], "held")
+        cast_wx(1, 0, nc.scalar.copy)
+        xq[0, 1] = quantize("xq01", xb[0, 1], "b16")
+        wq[0, 0] = quantize("wq00", wb[0, 0], "b16")
         gather(1, 3, 0, 0, 256)
         interleave(1, 0, 0, 256)
         gather(1, 3, 0, 256, 512)

@@ -231,9 +231,9 @@ def tile_list_relation_type_max_kernel(
             if (c, b) not in hb:
                 hb[c, b] = tagged("b16", [P, CH * PACK], BF16)
             nc.vector.tensor_tensor(
-                hb[c, b][:, PACK * lo : PACK * hi].rearrange("p (c i t) -> p c t i", i=4, t=PACK),
-                p_sb[c, b][:, :, lo:hi].rearrange("p t (c i) -> p c t i", i=4),
-                biased[c, b][:, :, lo:hi].rearrange("p t (c i) -> p c t i", i=4),
+                hb[c, b][:, PACK * lo : PACK * hi].rearrange("p (c i t) -> p c t i", i=8, t=PACK),
+                p_sb[c, b][:, :, lo:hi].rearrange("p t (c i) -> p c t i", i=8),
+                biased[c, b][:, :, lo:hi].rearrange("p t (c i) -> p c t i", i=8),
                 ALU.max,
             )
 
@@ -242,9 +242,9 @@ def tile_list_relation_type_max_kernel(
             if q not in hb:
                 hb[q] = tagged("b16", [P, 2, QT * PACK], BF16)
             nc.vector.tensor_tensor(
-                hb[q][:, b, :].rearrange("p (c i t) -> p c t i", i=4, t=PACK),
-                p_sb[c, b][:, :, lo : lo + QT].rearrange("p t (c i) -> p c t i", i=4),
-                biased[c, b][:, :, lo : lo + QT].rearrange("p t (c i) -> p c t i", i=4),
+                hb[q][:, b, :].rearrange("p (c i t) -> p c t i", i=8, t=PACK),
+                p_sb[c, b][:, :, lo : lo + QT].rearrange("p t (c i) -> p c t i", i=8),
+                biased[c, b][:, :, lo : lo + QT].rearrange("p t (c i) -> p c t i", i=8),
                 ALU.max,
             )
 

@@ -195,19 +195,22 @@ def tile_list_relation_type_max_kernel(
         def project_x(c, b, lo=0, hi=CH):
             if (c, b) not in biased:
                 biased[c, b] = tagged("f32x4", [P, PACK, CH], F32)
-            for t in range(PACK):
-                acc = psum.tile([P, hi - lo], F32, name="acc", bufs=bufs["acc"])
-                for a in range(2):
-                    nc.tensor.matmul_mx(
-                        out=acc[:],
-                        lhsT=wq[a, b][0][:, P * t : P * (t + 1)].bitcast(FP8X4),
-                        lhsT_scale=wq[a, b][1][:, P * t : P * (t + 1)],
-                        rhs=xq[a, c][0][:, lo:hi].bitcast(FP8X4),
-                        rhs_scale=xq[a, c][1][:, lo:hi],
-                        start=(a == 0),
-                        stop=(a == 1),
-                    )
-                nc.scalar.activation(biased[c, b][:, t, lo:hi], acc[:], ACT.Identity, bias=bx_sb[:, b, t : t + 1])
+            for first in range(0, PACK, 2):
+                acc = {}
+                for t in (first + 1, first):
+                    acc[t] = psum.tile([P, hi - lo], F32, name="acc", bufs=bufs["acc"])
+                    for a in range(2):
+                        nc.tensor.matmul_mx(
+                            out=acc[t][:],
+                            lhsT=wq[a, b][0][:, P * t : P * (t + 1)].bitcast(FP8X4),
+                            lhsT_scale=wq[a, b][1][:, P * t : P * (t + 1)],
+                            rhs=xq[a, c][0][:, lo:hi].bitcast(FP8X4),
+                            rhs_scale=xq[a, c][1][:, lo:hi],
+                            start=(a == 0),
+                            stop=(a == 1),
+                        )
+                for t in (first, first + 1):
+                    nc.scalar.activation(biased[c, b][:, t, lo:hi], acc[t][:], ACT.Identity, bias=bx_sb[:, b, t : t + 1])
 
         p_sb = {}
 
@@ -355,9 +358,9 @@ def tile_list_relation_type_max_kernel(
         interleave(1, 0, 256, 512)
         gather(1, 3, 1)
         interleave(1, 1)
-        cast_wx(0, 1, nc.vector.tensor_copy)
         wq[1, 0] = quantize("wq10", wb[1, 0], "b16")
         xq[1, 0] = quantize("xq10", xb[1, 0][:, 0:1024], "b16", 0, 256)
+        cast_wx(0, 1, nc.vector.tensor_copy)
         quantize("xq10", xb[1, 0][:, 1024:2048], "b16", 256, CH)
         cast_wx(1, 1, nc.vector.tensor_copy)
         wq[0, 1] = quantize("wq01", wb[0, 1], "b16")

@@ -357,24 +357,27 @@ def tile_list_relation_type_max_kernel(
         gather(1, 3, 0, 256, 512)
         interleave(1, 0, 256, 512)
         gather(1, 3, 1)
-        interleave(1, 1)
+        interleave(1, 1, 0, QT)
         wq[1, 0] = quantize("wq10", wb[1, 0], "b16")
         xq[1, 0] = quantize("xq10", xb[1, 0][:, 0:1024], "b16", 0, 256)
-        cast_wx(0, 1, nc.vector.tensor_copy)
+        cast_wx(0, 1, nc.vector.tensor_copy, 0, KP - P)
+        cast_wx(0, 1, nc.scalar.copy, KP - P, KP)
         quantize("xq10", xb[1, 0][:, 1024:2048], "b16", 256, CH)
         cast_wx(1, 1, nc.vector.tensor_copy)
         wq[0, 1] = quantize("wq01", wb[0, 1], "b16")
         wq[1, 1] = quantize("wq11", wb[1, 1], "codes")
-        xq[1, 1] = quantize("xq11", xb[1, 1], "codes")
+        xq[1, 1] = quantize("xq11", xb[1, 1][:, 0:1024], "codes", 0, 256)
         project_x(0, 0, 0, 256)
         project_x(0, 0, 256, 512)
         project_x(0, 1, 0, 256)
         project_x(0, 1, 256, 512)
+        interleave(1, 1, QT, CH)
         join(0, 0, 0, 256)
         join(0, 0, 256, 512)
         join(0, 1, 0, 256)
         quantize_h(0, 0, "codes")
         join(0, 1, 256, 512)
+        quantize("xq11", xb[1, 1][:, 1024:2048], "codes", 256, CH)
         project_x(1, 0, 0, 256)
         project_x(1, 1, 0, 256)
         join_quarter(2, 0)

from contextlib import ExitStack

import concourse.mybir as mybir
from concourse.masks import make_identity

K, D, H, N, T, V, S = 1024, 512, 1024, 512, 2048, 2048, 1024
FLOPS = 2 * S * (K * H + D * H + H * N)

F32 = mybir.dt.float32
BF16 = mybir.dt.bfloat16
I32 = mybir.dt.int32
U32 = mybir.dt.uint32
U16 = mybir.dt.uint16
U8 = mybir.dt.uint8
FP8X4 = mybir.dt.float8_e4m3fn_x4
FP4X4 = mybir.dt.float4_e2m1fn_x4
ALU = mybir.AluOpType
ACT = mybir.ActivationFunctionType

P = 128
PACK = 4
KP = P * PACK
CH = 512
NCH = S // CH
R, GROUP = 8, 16
NB = S // P
QT = 256


def tile_list_relation_type_max_kernel(
    tc, xT, wgt, offs2, tab_words, tab_scales, offs, wx, bx, wt_words, wt_scales, wo_words, wo_scales, bo, old, out
):
    nc = tc.nc
    with ExitStack() as ctx:
        lists = ctx.enter_context(tc.tile_pool(name="lists", bufs=1))
        keep = ctx.enter_context(tc.tile_pool(name="keep", bufs=1))
        ring = ctx.enter_context(tc.tile_pool(name="ring", bufs=2))
        psum = ctx.enter_context(tc.psum_pool(name="psum", bufs=1))
        bufs = {"plane": 5, "wx_raw": 4, "b16": 10, "tgs": 2, "codes": 10, "pair": 2, "f32x4": 4, "p_sb": 4, "th": 5, "acc": 8}

        def kept(name, shape, dtype):
            return keep.tile(shape, dtype, name=name, align_bytes=64)

        def tagged(tag, shape, dtype):
            return ring.tile(shape, dtype, name=tag, bufs=bufs[tag], align_bytes=64)

        offs2_sb = lists.tile([P, S // 16], U16, name="offs2_sb")
        offs_sb = lists.tile([P, S // 16], U16, name="offs_sb")

        wt_sc_raw = kept("wt_sc_raw", [P, H // 4], I32)
        tab_sc = kept("tab_sc", [P, V // 4], I32)
        wo_sc = kept("wo_sc", [P, 2, N // 4], I32)
        nc.vector.memset(tab_sc[:], 0)
        nc.vector.memset(wt_sc_raw[:], 0)
        nc.vector.memset(wo_sc[:], 0)
        bx_sb = kept("bx_sb", [P, 2, PACK], F32)
        bo_sb = kept("bo_sb", [P, N // P], F32)

        def load_scale_rows(tile, rows):
            for r in range(4):
                nc.sync.dma_start(tile[r:P:32], rows[r:16:4].bitcast(I32))

        wt_raw = kept("wt_raw", [P, H // 2], I32)
        wgt_sb = kept("wgt_sb", [P, S], F32)
        tab_w = tagged("plane", [P, V], I32)
        wo_w = kept("wo_w", [P, 2, N], I32)
        old_sb, planes, wx_raw = {}, {}, {}

        w_rows = kept("w_rows", [P, P], F32)
        ident = kept("ident", [P, P], F32)

        def load_edge_weights():
            nc.gpsimd.memset(w_rows[R * NB : P, :], 0.0)
            make_identity(nc, ident[:])
            nc.sync.dma_start(w_rows[0 : R * NB, :], wgt[0:P:GROUP, :].rearrange("g (b j) -> g b j", j=P))

        def spread_edge_weights():
            turned = psum.tile([P, P], F32, name="acc", bufs=bufs["acc"])
            nc.tensor.transpose(turned[:], w_rows[:], ident[:])
            by_block = turned[:, 0 : R * NB].rearrange("j (g b) -> j b g", b=NB)
            for c in range(NCH):
                wide = tagged("pair", [P, PACK, R, GROUP], F32)
                nc.scalar.copy(wide[:], by_block[:, PACK * c : PACK * (c + 1), :].unsqueeze(3).to_broadcast([P, PACK, R, GROUP]))
                back = psum.tile([P, PACK, P], F32, name="acc", bufs=bufs["acc"])
                for k in range(PACK):
                    nc.tensor.transpose(back[:, k, :], wide[:, k].rearrange("j g r -> j (g r)"), ident[:])
                nc.scalar.copy(wgt_sb[:, CH * c : CH * (c + 1)], back[:].rearrange("p k j -> p (k j)"))

        def load_plane(a, i, tag="plane"):
            planes[a, i] = tagged(tag, [P, T], F32)
            rows = xT[KP * a : KP * (a + 1), :].rearrange("(p i) t -> p i t", i=PACK)
            nc.sync.dma_start(planes[a, i][:], rows[:, i, :])

        def load_wx(a, b, lo=0, hi=KP):
            wx_raw[a, b, lo] = tagged("wx_raw", [P, PACK, hi - lo], F32)
            rows = wx[KP * a : KP * (a + 1), KP * b + lo : KP * b + hi].rearrange("(p j) c -> p j c", j=PACK)
            nc.sync.dma_start(wx_raw[a, b, lo][:], rows)

        def load_wx_rows(a, u):
            if a not in wx_raw:
                wx_raw[a] = kept("wx_rows", [P, PACK, H], F32)
                for b in range(2):
                    wx_raw[a, b, 0] = wx_raw[a][:, :, KP * b : KP * (b + 1)]
            rows = wx[KP * a : KP * (a + 1), :].rearrange("(p j) c -> p j c", j=PACK)
            nc.sync.dma_start(wx_raw[a][:, 2 * u : 2 * u + 2, :], rows[:, 2 * u : 2 * u + 2, :])

        def load_old(c):
            old_sb[c] = tagged("plane", [P, N // P, CH], F32)
            nc.sync.dma_start(old_sb[c][:], old[:, CH * c : CH * (c + 1)].rearrange("(c p) j -> p c j", p=P))

        wb, wq, xb, xq, g, tg_w = {}, {}, {}, {}, {}, {}

        def cast_wx(a, b, copy, lo=0, hi=KP):
            if (a, b) not in wb:
                wb[a, b] = tagged("b16", [P, KP * PACK], BF16)
            copy(
                wb[a, b][:].rearrange("p (t m j) -> p m j t", t=PACK, j=PACK)[:, lo // PACK : hi // PACK],
                wx_raw[a, b, 0][:, :, lo:hi].rearrange("p j (m t) -> p m j t", t=PACK),
            )

        made = {}

        def quantize(name, src, tag, lo=0, hi=CH):
            if name not in made:
                made[name] = tagged(tag, [P, CH], U32)[:], kept(name + "_s", [P, CH], U8)
            codes, scales = made[name]
            nc.vector.quantize_mx(
                out=codes[:, lo:hi].bitcast(FP8X4), scales=scales[:, lo:hi], in_=src[:]
            )
            return codes, scales

        def new_quad(a, c):
            quad = tagged("f32x4", [P, PACK, CH], F32)
            g[a, c] = quad
            for i in range(PACK):
                g[a, c, i] = quad[:, i, :]

        def new_pair(a, c, u):
            pair = tagged("pair", [P, 2, CH], F32)
            g[a, c, "pair", u] = pair
            for e in range(2):
                g[a, c, 2 * u + e] = pair[:, e, :]

        def gather(a, i, c, lo=0, hi=CH):
            nc.vector.tensor_tensor(
                g[a, c, i][:, lo:hi],
                planes[a, i][:].indirect(offs2_sb[:, (CH * c + lo) // 16 : (CH * c + hi) // 16]),
                wgt_sb[:, CH * c + lo : CH * c + hi],
                ALU.mult,
            )

        def interleave(a, c, lo=0, hi=CH, copy=nc.scalar.copy):
            if (a, c) not in xb:
                xb[a, c] = tagged("b16", [P, CH * PACK], BF16)
            copy(
                xb[a, c][:, PACK * lo : PACK * hi].rearrange("p (c i t) -> p c t i", i=4, t=PACK),
                g[a, c][:, :, lo:hi].rearrange("p t (c i) -> p c t i", i=4),
            )

        def interleave_pair(a, c, u, lo, hi):
            if (a, c) not in xb:
                xb[a, c] = tagged("b16", [P, CH * PACK], BF16)
            dst = xb[a, c][:, PACK * lo : PACK * hi].rearrange("p (n t) -> p n t", t=PACK)[:, :, 2 * u : 2 * u + 2]
            nc.scalar.copy(dst, g[a, c, "pair", u][:, :, lo:hi].rearrange("p t n -> p n t"))

        tg_s = {}

        def gather_tab_scales(c, tag):
            tg_s[c] = tagged(tag, [P, CH], U8)
            cols = slice(CH * c // 16, CH * (c + 1) // 16)
            nc.vector.tensor_copy(tg_s[c][:], tab_sc[:].bitcast(U8).indirect(offs_sb[:, cols]))

        def gather_tab_words(c, tag):
            tg_w[c] = tagged(tag, [P, CH], U32)
            cols = slice(CH * c // 16, CH * (c + 1) // 16)
            nc.vector.tensor_copy(tg_w[c][:], tab_w[:].bitcast(U32).indirect(offs_sb[:, cols]))

        wt_p = kept("wt_p", [P, 2 * H], U8)
        wt_sc = kept("wt_sc", [P, H], U8)

        def permute_wt_words():
            nc.gpsimd.tensor_copy(
                wt_p[:].bitcast(U16).rearrange("p (b t m) -> p b t m", b=2, t=PACK),
                wt_raw[:].bitcast(U16).rearrange("p (b m t) -> p b t m", b=2, t=PACK),
            )

        def permute_wt_scales(b):
            nc.gpsimd.tensor_copy(
                wt_sc[:, KP * b : KP * (b + 1)].rearrange("p (t m) -> p t m", t=PACK),
                wt_sc_raw[:].bitcast(U8)[:, KP * b : KP * (b + 1)].rearrange("p (m t) -> p t m", t=PACK),
            )

        hq, biased, hb = {}, {}, {}

        def project_x(c, b, lo=0, hi=CH):
            if (c, b) not in biased:
                biased[c, b] = tagged("f32x4", [P, PACK, CH], F32)
            for first in range(0, PACK, 2):
                acc = {}
                for t in (first + 1, first):
                    acc[t] = psum.tile([P, hi - lo], F32, name="acc", bufs=bufs["acc"])
                    for a in range(2):
                        nc.tensor.matmul_mx(
                            out=acc[t][:],
                            lhsT=wq[a, b][0][:, P * t : P * (t + 1)].bitcast(FP8X4),
                            lhsT_scale=wq[a, b][1][:, P * t : P * (t + 1)],
                            rhs=xq[a, c][0][:, lo:hi].bitcast(FP8X4),
                            rhs_scale=xq[a, c][1][:, lo:hi],
                            start=(a == 0),
                            stop=(a == 1),
                        )
                for t in (first, first + 1):
                    nc.scalar.activation(biased[c, b][:, t, lo:hi], acc[t][:], ACT.Identity, bias=bx_sb[:, b, t : t + 1])

        p_sb = {}

        def project_types(c, b):
            p_sb[c, b] = tagged("p_sb", [P, PACK, CH], F32)
            for t in range(PACK):
                col = KP * b + P * t
                acc = psum.tile([P, CH], F32, name="acc", bufs=bufs["acc"])
                nc.tensor.matmul_mx(
                    out=acc[:],
                    lhsT=wt_p[:, 2 * col : 2 * (col + P)].bitcast(FP4X4),
                    lhsT_scale=wt_sc[:, col : col + P],
                    rhs=tg_w[c][:].bitcast(FP8X4),
                    rhs_scale=tg_s[c][:],
                    start=True,
                    stop=True,
                )
                nc.scalar.copy(p_sb[c, b][:, t, :], acc[:])

        def join(c, b, lo=0, hi=CH):
            if (c, b) not in hb:
                hb[c, b] = tagged("b16", [P, CH * PACK], BF16)
            nc.vector.tensor_tensor(
                hb[c, b][:, PACK * lo : PACK * hi].rearrange("p (c i t) -> p c t i", i=8, t=PACK),
                p_sb[c, b][:, :, lo:hi].rearrange("p t (c i) -> p c t i", i=8),
                biased[c, b][:, :, lo:hi].rearrange("p t (c i) -> p c t i", i=8),
                ALU.max,
            )

        def join_quarter(q, b):
            c, lo = divmod(QT * q, CH)
            if q not in hb:
                hb[q] = tagged("b16", [P, 2, QT * PACK], BF16)
            nc.vector.tensor_tensor(
                hb[q][:, b, :].rearrange("p (c i t) -> p c t i", i=8, t=PACK),
                p_sb[c, b][:, :, lo : lo + QT].rearrange("p t (c i) -> p c t i", i=8),
                biased[c, b][:, :, lo : lo + QT].rearrange("p t (c i) -> p c t i", i=8),
                ALU.max,
            )

        def quantize_quarter(q):
            codes, scales = tagged("codes", [P, 2 * QT], U32), kept("hq_q%d_s" % q, [P, 2 * QT], U8)
            nc.vector.quantize_mx(out=codes[:].bitcast(FP8X4), scales=scales[:], in_=hb[q][:].rearrange("p b n -> p (b n)"))
            for b in range(2):
                hq["q", q, b] = codes[:, QT * b : QT * (b + 1)], scales[:, QT * b : QT * (b + 1)]

        def quantize_h(c, b, tag, lo=0, hi=CH):
            if (c, b) not in hq:
                hq[c, b] = tagged(tag, [P, CH], U32), kept("hq%d%d_s" % (c, b), [P, CH], U8)
            codes, scales = hq[c, b]
            nc.vector.quantize_mx(
                out=codes[:, lo:hi].bitcast(FP8X4), scales=scales[:, lo:hi], in_=hb[c, b][:, PACK * lo : PACK * hi]
            )

        th = {}

        def project_h(c, lo, hi, nts):
            th[c, lo, nts[0]] = tagged("th", [P, len(nts), hi - lo], F32)
            if c == 0:
                h_ops = [(hq[c, b][0][:, lo:hi], hq[c, b][1][:, lo:hi]) for b in range(2)]
            else:
                h_ops = [hq["q", (CH * c + lo) // QT, b] for b in range(2)]
            for k, nt in enumerate(nts):
                acc = psum.tile([P, hi - lo], F32, name="acc", bufs=bufs["acc"])
                for b in range(2):
                    nc.tensor.matmul_mx(
                        out=acc[:],
                        lhsT=wo_w[:, b, P * nt : P * (nt + 1)].bitcast(FP8X4),
                        lhsT_scale=wo_sc[:, b, :].bitcast(U8)[:, P * nt : P * (nt + 1)],
                        rhs=h_ops[b][0].bitcast(FP8X4),
                        rhs_scale=h_ops[b][1],
                        start=(b == 0),
                        stop=(b == 1),
                    )
                nc.scalar.activation(th[c, lo, nts[0]][:, k, :], acc[:], ACT.Tanh, bias=bo_sb[:, nt : nt + 1])

        def update(c, lo, hi, nts, adder, parts=1):
            rows = old_sb[c][:, nts[0] : nts[-1] + 1, lo:hi]
            step = (hi - lo) // parts
            for k in range(0, hi - lo, step):
                adder.tensor_tensor(rows[:, :, k : k + step], rows[:, :, k : k + step], th[c, lo, nts[0]][:, :, k : k + step], ALU.add)
            dst = out[P * nts[0] : P * (nts[-1] + 1), CH * c + lo : CH * c + hi].rearrange("(c p) j -> p c j", p=P)
            nc.sync.dma_start(dst, rows)

        nc.sync.dma_start(offs_sb[:], offs)
        nc.sync.dma_start(wt_raw[:], wt_words[0].bitcast(I32))
        load_edge_weights()
        load_scale_rows(tab_sc, tab_scales[0])
        nc.sync.dma_start(tab_w[:], tab_words[0].rearrange("p t i -> p (t i)").bitcast(I32))
        load_scale_rows(wt_sc_raw, wt_scales[0])
        nc.sync.dma_start(offs2_sb[:], offs2)
        load_plane(0, 0)
        load_plane(0, 1)
        load_plane(0, 2)
        load_plane(0, 3)
        load_plane(1, 0)
        load_wx(0, 0)
        load_plane(1, 1)
        load_plane(1, 2)
        load_wx(1, 0)
        load_plane(1, 3)
        load_wx(0, 1)
        load_wx(1, 1)
        nc.sync.dma_start(bx_sb[:], bx.rearrange("(b p t) -> p b t", b=2, t=PACK))
        load_scale_rows(wo_sc, wo_scales.rearrange("a r n -> r a n"))
        nc.sync.dma_start(wo_w[:], wo_words.rearrange("a p n t -> p a (n t)").bitcast(I32))
        with nc.allow_non_contiguous_dma(reason="one bias value to a partition"):
            nc.sync.dma_start(bo_sb[:], bo.rearrange("(c p) -> p c", p=P))
        spread_edge_weights()
        permute_wt_words()
        gather_tab_scales(0, "tgs")
        gather_tab_scales(1, "tgs")
        permute_wt_scales(0)
        permute_wt_scales(1)
        gather_tab_words(0, "codes")
        gather_tab_words(1, "codes")
        for b in range(2):
            for c in range(NCH):
                project_types(c, b)
        new_quad(0, 0)
        new_quad(0, 1)
        for i in range(PACK):
            gather(0, i, 0)
            gather(0, i, 1)
        load_old(0)
        load_old(1)
        interleave(0, 0)
        interleave(0, 1)
        cast_wx(0, 0, nc.scalar.copy)
        new_quad(1, 0)
        new_quad(1, 1)
        gather(1, 0, 0)
        gather(1, 0, 1)
        xq[0, 0] = quantize("xq00", xb[0, 0], "codes")
        gather(1, 1, 0)
        gather(1, 1, 1)
        gather(1, 2, 0)
        gather(1, 2, 1)
        cast_wx(1, 0, nc.scalar.copy)
        xq[0, 1] = quantize("xq01", xb[0, 1], "b16")
        wq[0, 0] = quantize("wq00", wb[0, 0], "b16")
        gather(1, 3, 0, 0, 256)
        interleave(1, 0, 0, 256)
        gather(1, 3, 0, 256, 512)
        interleave(1, 0, 256, 512)
        gather(1, 3, 1)
        interleave(1, 1, 0, QT)
        wq[1, 0] = quantize("wq10", wb[1, 0], "b16")
        xq[1, 0] = quantize("xq10", xb[1, 0][:, 0:1024], "b16", 0, 256)
        cast_wx(0, 1, nc.vector.tensor_copy, 0, KP - P)
        cast_wx(0, 1, nc.scalar.copy, KP - P, KP)
        quantize("xq10", xb[1, 0][:, 1024:2048], "b16", 256, CH)
        cast_wx(1, 1, nc.vector.tensor_copy)
        wq[0, 1] = quantize("wq01", wb[0, 1], "b16")
        wq[1, 1] = quantize("wq11", wb[1, 1], "codes")
        xq[1, 1] = quantize("xq11", xb[1, 1][:, 0:1024], "codes", 0, 256)
        project_x(0, 0, 0, 256)
        project_x(0, 0, 256, 512)
        project_x(0, 1, 0, 256)
        project_x(0, 1, 256, 512)
        interleave(1, 1, QT, CH)
        join(0, 0, 0, 256)
        join(0, 0, 256, 512)
        join(0, 1, 0, 256)
        quantize_h(0, 0, "codes")
        join(0, 1, 256, 512)
        quantize("xq11", xb[1, 1][:, 1024:2048], "codes", 256, CH)
        project_x(1, 0, 0, 256)
        project_x(1, 1, 0, 256)
        join_quarter(2, 0)
        quantize_h(0, 1, "codes")
        project_x(1, 0, 256, 512)
        project_x(1, 1, 256, 512)
        join_quarter(2, 1)
        project_h(0, 0, CH, [0])
        project_h(0, 0, CH, [1])
        join_quarter(3, 0)
        quantize_quarter(2)
        project_h(0, 0, CH, [2])
        project_h(0, 0, CH, [3])
        join_quarter(3, 1)
        update(0, 0, CH, [0], nc.vector)
        quantize_quarter(3)
        project_h(1, 0, QT, [0, 1])
        project_h(1, 0, QT, [2, 3])
        update(0, 0, CH, [1], nc.vector)
        update(0, 0, CH, [2], nc.vector)
        update(0, 0, CH, [3], nc.vector)
        update(1, 0, QT, [0, 1], nc.vector)
        update(1, 0, QT, [2, 3], nc.vector)
        project_h(1, QT, CH, [0, 1])
        update(1, QT, CH, [0, 1], nc.vector)
        project_h(1, QT, CH, [2])
        update(1, QT, CH, [2], nc.vector)
        project_h(1, QT, CH, [3])
        update(1, QT, CH, [3], nc.vector)
